import numpy as np
import ml_dtypes


def mxq(x, axis, fmt="e4m3"):
    dtype, down = {"e4m3": (ml_dtypes.float8_e4m3fn, 7), "e5m2": (ml_dtypes.float8_e5m2, 14)}[fmt]
    v = np.moveaxis(np.asarray(x, np.float32).astype(ml_dtypes.bfloat16).astype(np.float64), axis, -1)
    blocks = v.reshape(v.shape[:-1] + (-1, 32))
    amax = np.abs(blocks).max(-1, keepdims=True)
    byte = np.maximum(np.where(amax > 0, np.frexp(amax)[1] - 1 + 127, 0) - down, 1)
    scale = np.exp2(byte - 127.0)
    codes = (blocks / scale).astype(np.float32).astype(dtype).astype(np.float64)
    return np.moveaxis((codes * scale).reshape(v.shape), -1, axis)


WIDE = False


def mx_kscale(k):
    if not WIDE:
        return np.ones(k)
    levels = np.array([10, -10, 5, -5, 0])
    if k % 512:
        return np.exp2(np.random.permutation(np.resize(levels, k // 32))).repeat(32)
    a = np.empty((k // 512, 16))
    for p in range(k // 512):
        a[p, :8] = np.random.permutation(np.resize(levels, 8))
        for g in range(8):
            far = levels[np.abs(levels - a[p, g]) >= 10]
            a[p, g + 8] = far[np.random.randint(len(far))]
    return np.exp2(a.ravel()).repeat(32)


def f64(x):
    return np.asarray(x).astype(np.float64)


def striped(idx):
    return np.tile(idx.reshape(-1, 16).T, (8, 1)).astype(np.uint16)


def unstriped(offs):
    return offs[:16].T.reshape(-1).astype(np.int64)


K, T, S, N, U = 1024, 1024, 512, 128, 1024
P = 2 ** 7


def setup_inputs():
    n = np.random.standard_normal
    s = mx_kscale(K)[:, None]
    return {
        "xT": (n((K, T)) * s).astype(np.float32),
        "mem": n((N, U)).astype(np.float32),
        "w1": (n((K, N)) / np.sqrt(K) / s).astype(np.float32),
        "old": np.tile(np.random.uniform(0.5, 0.95, S), (P, 1)).astype(np.float32),
        "new": np.tile(np.random.uniform(0.05, 0.5, S), (P, 1)).astype(np.float32),
        "offs": striped(np.random.permutation(T)[:S]),
        "slot": striped(np.random.permutation(U)[:S]),
    }


def reference(xT, mem, w1, old, new, offs, slot):
    xq = mxq(f64(xT)[:, unstriped(offs)], 0, "e4m3")
    y = np.tanh(mxq(f64(w1), 0, "e4m3").T @ xq)
    out = f64(mem).copy()
    out[:, unstriped(slot)] = f64(mem)[:, unstriped(slot)] * f64(old)[:1] + y * f64(new)[:1]
    return out

@@ -1,0 +1,166 @@
+from contextlib import ExitStack
+
+import concourse.mybir as mybir
+from concourse.masks import make_identity
+
+K, T, S, M, U = 1024, 1024, 512, 128, 1024
+FLOPS = 2 * K * M * S
+
+F32 = mybir.dt.float32
+BF16 = mybir.dt.bfloat16
+U32 = mybir.dt.uint32
+I32 = mybir.dt.int32
+U16 = mybir.dt.uint16
+U8 = mybir.dt.uint8
+FP8X4 = mybir.dt.float8_e4m3fn_x4
+MULT = mybir.AluOpType.mult
+ADD = mybir.AluOpType.add
+TANH = mybir.ActivationFunctionType.Tanh
+
+P = 128
+PACK = 4
+PASSES = K // (P * PACK)
+LIST = 16
+SLICE = 128
+SLICES = S // SLICE
+LOADS = [[(0, 1024, 384)], [(0, 1024, 576)], [(0, 1024, 704)], [(0, 512, 512), (512, 512, 256)]]
+SCATTERS = [(2, 0, 256), (3, 256, 512)]
+
+
+def tile_picked_ema_tanh_e_kernel(tc, xT, mem, w1, old, new, offs, slot, out):
+    nc = tc.nc
+    with ExitStack() as ctx:
+        held = ctx.enter_context(tc.tile_pool(name="held", bufs=1))
+        psum = ctx.enter_context(tc.psum_pool(name="psum", bufs=1))
+
+        offs_t = held.tile([P, S // LIST], U16, name="offs_t")
+        slot_t = held.tile([P, S // LIST], U16, name="slot_t")
+        mem_t = held.tile([P, U], F32, name="mem_t", align_bytes=64)
+        old_col = held.tile([P, PACK], F32, name="old_col")
+        new_t = held.tile([P, S], F32, name="new_t", align_bytes=64)
+        warm = held.tile([P, 8], F32, name="warm")
+        ident = held.tile([P, P], F32, name="ident", align_bytes=64)
+
+        x_rows = xT.rearrange("(z p u e) t -> z u p e t", z=PASSES, p=P, u=2, e=2)
+        w_rows = w1.rearrange("(z p j) m -> z p j m", z=PASSES, p=P, j=PACK)
+
+        raw = {}
+
+        def load_x(q, c):
+            t0, n, unused = LOADS[q][c]
+            raw[q, c] = held.tile([P, 2, n], F32, name=f"raw{q}_{c}", align_bytes=64)
+            nc.sync.dma_start(raw[q, c][:], x_rows[q // 2, q % 2][:, :, t0 : t0 + n])
+
+        nc.sync.dma_start(old_col[:], old[0:1, :].rearrange("o (p c) -> (o p) c", c=PACK))
+        nc.sync.dma_start(mem_t[:], mem)
+        nc.sync.dma_start(slot_t[:], slot)
+        load_x(0, 0)
+        nc.sync.dma_start(offs_t[:], offs)
+        for q in range(2 * PASSES):
+            for c in range(len(LOADS[q])):
+                if (q, c) != (0, 0):
+                    load_x(q, c)
+        w_raw = []
+        for z in range(PASSES):
+            w_raw.append(held.tile([P, PACK, M], F32, name=f"w_raw{z}", align_bytes=64))
+            nc.sync.dma_start(w_raw[z][:], w_rows[z])
+        nc.sync.dma_start(new_t[:], new)
+
+        nc.gpsimd.memset(warm[:], 0.0)
+        nc.scalar.activation(warm[:, 0:1], warm[:, 1:2], TANH)
+        make_identity(nc, ident[:])
+
+        old_ps = psum.tile([P, PACK, P], F32, name="old_ps")
+        for c in range(PACK):
+            nc.tensor.transpose(old_ps[:, c, :], old_col[:, c : c + 1].to_broadcast([P, P]), ident[:])
+        found = held.tile([P, S], F32, name="found", align_bytes=64)
+        nc.vector.tensor_copy(found[:], mem_t[:].indirect(slot_t[:]))
+        kept = held.tile([P, S], F32, name="kept", align_bytes=64)
+        nc.vector.tensor_tensor(
+            kept[:].rearrange("p (n c) -> p n c", c=PACK),
+            found[:].rearrange("p (n c) -> p n c", c=PACK),
+            old_ps[:].rearrange("p c n -> p n c"),
+            MULT,
+        )
+
+        pairs = [held.tile([P, 2 * T], BF16, name=f"pairs{q}", align_bytes=64) for q in range(2 * PASSES)]
+
+        def cast(q):
+            for c, (t0, n, ns) in enumerate(LOADS[q]):
+                src = raw[q, c][:].rearrange("p e t -> p t e")
+                dst = pairs[q][:, 2 * t0 : 2 * (t0 + n)].rearrange("p (t e) -> p t e", e=2)
+                if ns > 0:
+                    nc.scalar.copy(dst[:, 0:ns, :], src[:, 0:ns, :])
+                if ns < n:
+                    nc.vector.tensor_copy(dst[:, ns:n, :], src[:, ns:n, :])
+
+        def gather(q, halves, j0, n):
+            window = pairs[q][:].bitcast(U32)
+            nc.vector.tensor_copy(halves[:, q % 2, :], window.indirect(offs_t[:, j0 // LIST : (j0 + n) // LIST]))
+
+        def weave(picked, halves):
+            words = picked[:].bitcast(I32).rearrange("p (j u) -> p j u", u=2)
+            nc.vector.tensor_copy(words, halves[:].bitcast(I32).rearrange("p u j -> p j u"))
+
+        def quantize(src, n, name):
+            codes = held.tile([P, n], U32, name=name + "_codes", align_bytes=64)
+            scales = held.tile([P, n], U8, name=name + "_scales", align_bytes=64)
+            nc.vector.quantize_mx(out=codes[:].bitcast(FP8X4), scales=scales[:], in_=src[:])
+            return codes, scales
+
+        picked0 = held.tile([P, PACK * S], BF16, name="picked0", align_bytes=64)
+        picked1 = [held.tile([P, PACK * SLICE], BF16, name=f"picked1_{s}", align_bytes=64) for s in range(SLICES)]
+        halves0 = held.tile([P, 2, S], U32, name="halves0", align_bytes=64)
+        halves1 = [held.tile([P, 2, SLICE], U32, name=f"halves1_{s}", align_bytes=64) for s in range(SLICES)]
+        cast(0)
+        gather(0, halves0, 0, S)
+        cast(1)
+        gather(1, halves0, 0, S)
+        cast(2)
+        weave(picked0, halves0)
+        gather(2, halves1[0], 0, SLICE)
+        x0 = quantize(picked0, S, "x0")
+        for s in range(1, SLICES):
+            gather(2, halves1[s], s * SLICE, SLICE)
+        cast(3)
+
+        w_grouped = held.tile([P, PASSES * M * PACK], BF16, name="w_grouped", align_bytes=64)
+        for z in range(PASSES):
+            dst = w_grouped[:, z * M * PACK : (z + 1) * M * PACK].rearrange("p (c i j) -> p c j i", i=4, j=PACK)
+            nc.scalar.copy(dst, w_raw[z][:].rearrange("p j (c i) -> p c j i", i=4))
+
+        x1 = {}
+        for step in range(SLICES + 2):
+            if step < SLICES:
+                gather(3, halves1[step], step * SLICE, SLICE)
+            if step == 4:
+                w_codes, w_scales = quantize(w_grouped, PASSES * M, "w")
+            if 1 <= step <= SLICES:
+                weave(picked1[step - 1], halves1[step - 1])
+            if step >= 2:
+                x1[step - 2] = quantize(picked1[step - 2], SLICE, f"x1_{step - 2}")
+
+        moved = held.tile([P, S], F32, name="moved", align_bytes=64)
+        for s in range(SLICES):
+            cols = slice(s * SLICE, (s + 1) * SLICE)
+            acc = psum.tile([P, SLICE], F32, name=f"acc{s}")
+            rhs = [(x0[0][:, cols], x0[1][:, cols]), (x1[s][0][:], x1[s][1][:])]
+            for z in range(PASSES):
+                nc.tensor.matmul_mx(
+                    out=acc[:],
+                    lhsT=w_codes[:, z * M : (z + 1) * M].bitcast(FP8X4),
+                    lhsT_scale=w_scales[:, z * M : (z + 1) * M],
+                    rhs=rhs[z][0].bitcast(FP8X4),
+                    rhs_scale=rhs[z][1],
+                    start=(z == 0),
+                    stop=(z == PASSES - 1),
+                )
+            y = held.tile([P, SLICE], F32, name=f"y{s}", align_bytes=64)
+            nc.scalar.activation(y[:], acc[:], TANH)
+            nc.vector.tensor_tensor(moved[:, cols], y[:], new_t[:, cols], MULT)
+            for after, a, b in SCATTERS:
+                if after == s:
+                    nc.vector.tensor_tensor(
+                        mem_t[:].indirect(slot_t[:, a // LIST : b // LIST]), moved[:, a:b], kept[:, a:b], ADD
+                    )
+        nc.sync.dma_start(out, mem_t[:])

@@ -8,8 +8,8 @@ FLOPS = 2 * K * M * S
 
 F32 = mybir.dt.float32
 BF16 = mybir.dt.bfloat16
-U32 = mybir.dt.uint32
 I32 = mybir.dt.int32
+U32 = mybir.dt.uint32
 U16 = mybir.dt.uint16
 U8 = mybir.dt.uint8
 FP8X4 = mybir.dt.float8_e4m3fn_x4
@@ -21,17 +21,16 @@ P = 128
 PACK = 4
 PASSES = K // (P * PACK)
 LIST = 16
-SLICE = 128
-SLICES = S // SLICE
-LOADS = [[(0, 1024, 384)], [(0, 1024, 576)], [(0, 1024, 704)], [(0, 512, 512), (512, 512, 256)]]
-SCATTERS = [(2, 0, 256), (3, 256, 512)]
+SLICES = [(0, 128), (128, 256), (256, 512)]
+LOADS = [[(0, 1024, 448)], [(0, 1024, 448)], [(0, 512, 512), (512, 512, 512)], [(0, 512, 512), (512, 512, 256)]]
 
 
 def tile_picked_ema_tanh_e_kernel(tc, xT, mem, w1, old, new, offs, slot, out):
     nc = tc.nc
     with ExitStack() as ctx:
         held = ctx.enter_context(tc.tile_pool(name="held", bufs=1))
-        psum = ctx.enter_context(tc.psum_pool(name="psum", bufs=1))
+        sums = ctx.enter_context(tc.psum_pool(name="sums", bufs=1))
+        turns = ctx.enter_context(tc.psum_pool(name="turns", bufs=4))
 
         offs_t = held.tile([P, S // LIST], U16, name="offs_t")
         slot_t = held.tile([P, S // LIST], U16, name="slot_t")
@@ -51,7 +50,7 @@ def tile_picked_ema_tanh_e_kernel(tc, xT, mem, w1, old, new, offs, slot, out):
             raw[q, c] = held.tile([P, 2, n], F32, name=f"raw{q}_{c}", align_bytes=64)
             nc.sync.dma_start(raw[q, c][:], x_rows[q // 2, q % 2][:, :, t0 : t0 + n])
 
-        nc.sync.dma_start(old_col[:], old[0:1, :].rearrange("o (p c) -> (o p) c", c=PACK))
+        nc.scalar.dma_start(old_col[:], old[0:1, :].rearrange("o (p c) -> (o p) c", c=PACK))
         nc.sync.dma_start(mem_t[:], mem)
         nc.sync.dma_start(slot_t[:], slot)
         load_x(0, 0)
@@ -62,7 +61,7 @@ def tile_picked_ema_tanh_e_kernel(tc, xT, mem, w1, old, new, offs, slot, out):
                     load_x(q, c)
         w_raw = []
         for z in range(PASSES):
-            w_raw.append(held.tile([P, PACK, M], F32, name=f"w_raw{z}", align_bytes=64))
+            w_raw.append(held.tile([P, PACK, M], F32, name=f"w_raw{z}", tag=f"w_raw{z}", align_bytes=64))
             nc.sync.dma_start(w_raw[z][:], w_rows[z])
         nc.sync.dma_start(new_t[:], new)
 
@@ -70,7 +69,7 @@ def tile_picked_ema_tanh_e_kernel(tc, xT, mem, w1, old, new, offs, slot, out):
         nc.scalar.activation(warm[:, 0:1], warm[:, 1:2], TANH)
         make_identity(nc, ident[:])
 
-        old_ps = psum.tile([P, PACK, P], F32, name="old_ps")
+        old_ps = turns.tile([P, PACK, P], F32, name="old_ps", tag="turn")
         for c in range(PACK):
             nc.tensor.transpose(old_ps[:, c, :], old_col[:, c : c + 1].to_broadcast([P, P]), ident[:])
         found = held.tile([P, S], F32, name="found", align_bytes=64)
@@ -94,73 +93,79 @@ def tile_picked_ema_tanh_e_kernel(tc, xT, mem, w1, old, new, offs, slot, out):
                 if ns < n:
                     nc.vector.tensor_copy(dst[:, ns:n, :], src[:, ns:n, :])
 
-        def gather(q, halves, j0, n):
+        def gather(q, target, j0, n):
             window = pairs[q][:].bitcast(U32)
-            nc.vector.tensor_copy(halves[:, q % 2, :], window.indirect(offs_t[:, j0 // LIST : (j0 + n) // LIST]))
+            nc.vector.tensor_copy(target, window.indirect(offs_t[:, j0 // LIST : (j0 + n) // LIST]))
 
         def weave(picked, halves):
             words = picked[:].bitcast(I32).rearrange("p (j u) -> p j u", u=2)
             nc.vector.tensor_copy(words, halves[:].bitcast(I32).rearrange("p u j -> p j u"))
 
-        def quantize(src, n, name):
-            codes = held.tile([P, n], U32, name=name + "_codes", align_bytes=64)
+        def quantize(src, n, name, tag):
+            codes = held.tile([P, n], U32, name=name + "_codes", tag=tag, align_bytes=64)
             scales = held.tile([P, n], U8, name=name + "_scales", align_bytes=64)
             nc.vector.quantize_mx(out=codes[:].bitcast(FP8X4), scales=scales[:], in_=src[:])
             return codes, scales
 
         picked0 = held.tile([P, PACK * S], BF16, name="picked0", align_bytes=64)
-        picked1 = [held.tile([P, PACK * SLICE], BF16, name=f"picked1_{s}", align_bytes=64) for s in range(SLICES)]
+        halves1 = [held.tile([P, 2, b - a], U32, name=f"halves1_{a}", align_bytes=64) for a, b in SLICES]
         halves0 = held.tile([P, 2, S], U32, name="halves0", align_bytes=64)
-        halves1 = [held.tile([P, 2, SLICE], U32, name=f"halves1_{s}", align_bytes=64) for s in range(SLICES)]
         cast(0)
-        gather(0, halves0, 0, S)
+        gather(0, halves0[:, 0, :], 0, S)
         cast(1)
-        gather(1, halves0, 0, S)
-        cast(2)
+        gather(1, halves0[:, 1, :], 0, S)
         weave(picked0, halves0)
-        gather(2, halves1[0], 0, SLICE)
-        x0 = quantize(picked0, S, "x0")
-        for s in range(1, SLICES):
-            gather(2, halves1[s], s * SLICE, SLICE)
+        cast(2)
+        x0 = quantize(picked0, S, "x0", "x0_codes")
+        for s, (a, b) in enumerate(SLICES):
+            gather(2, halves1[s][:, 0, :], a, b - a)
         cast(3)
 
-        w_grouped = held.tile([P, PASSES * M * PACK], BF16, name="w_grouped", align_bytes=64)
+        w_grouped = []
         for z in range(PASSES):
-            dst = w_grouped[:, z * M * PACK : (z + 1) * M * PACK].rearrange("p (c i j) -> p c j i", i=4, j=PACK)
+            w_grouped.append(held.tile([P, M * PACK], BF16, name=f"w_grouped{z}", tag=f"w_grouped{z}", align_bytes=64))
+            dst = w_grouped[z][:].rearrange("p (c i j) -> p c j i", i=4, j=PACK)
             nc.scalar.copy(dst, w_raw[z][:].rearrange("p j (c i) -> p c j i", i=4))
 
-        x1 = {}
-        for step in range(SLICES + 2):
-            if step < SLICES:
-                gather(3, halves1[step], step * SLICE, SLICE)
-            if step == 4:
-                w_codes, w_scales = quantize(w_grouped, PASSES * M, "w")
-            if 1 <= step <= SLICES:
-                weave(picked1[step - 1], halves1[step - 1])
-            if step >= 2:
-                x1[step - 2] = quantize(picked1[step - 2], SLICE, f"x1_{step - 2}")
+        for s, (a, b) in enumerate(SLICES):
+            gather(3, halves1[s][:, 1, :], a, b - a)
 
-        moved = held.tile([P, S], F32, name="moved", align_bytes=64)
-        for s in range(SLICES):
-            cols = slice(s * SLICE, (s + 1) * SLICE)
-            acc = psum.tile([P, SLICE], F32, name=f"acc{s}")
-            rhs = [(x0[0][:, cols], x0[1][:, cols]), (x1[s][0][:], x1[s][1][:])]
+        def woven(s, tag):
+            a, b = SLICES[s]
+            picked = held.tile([P, PACK * (b - a)], BF16, name=f"picked1_{s}", tag=tag, align_bytes=64)
+            weave(picked, halves1[s])
+            return picked
+
+        first = woven(0, "picked1_0")
+        wq = [quantize(w_grouped[0], M, "w0", "w0_codes")]
+        x1 = [quantize(first, SLICES[0][1], "x1_0", "w_grouped0")]
+        wq.append(quantize(w_grouped[1], M, "w1", "w1_codes"))
+        rest = [woven(1, "w_grouped1"), woven(2, "w_raw1")]
+        for s in (1, 2):
+            x1.append(quantize(rest[s - 1], SLICES[s][1] - SLICES[s][0], f"x1_{s}", f"x1_{s}_codes"))
+
+        y = held.tile([P, S], F32, name="y", align_bytes=64)
+
+        def move(a, b):
+            moved = held.tile([P, b - a], F32, name=f"moved{a}", align_bytes=64)
+            nc.vector.tensor_tensor(moved[:], y[:, a:b], new_t[:, a:b], MULT)
+            nc.vector.tensor_tensor(mem_t[:].indirect(slot_t[:, a // LIST : b // LIST]), moved[:], kept[:, a:b], ADD)
+
+        for s, (a, b) in enumerate(SLICES):
+            acc = sums.tile([P, b - a], F32, name=f"acc{s}")
+            xq = [(x0[0][:, a:b], x0[1][:, a:b]), (x1[s][0][:], x1[s][1][:])]
             for z in range(PASSES):
                 nc.tensor.matmul_mx(
                     out=acc[:],
-                    lhsT=w_codes[:, z * M : (z + 1) * M].bitcast(FP8X4),
-                    lhsT_scale=w_scales[:, z * M : (z + 1) * M],
-                    rhs=rhs[z][0].bitcast(FP8X4),
-                    rhs_scale=rhs[z][1],
+                    lhsT=wq[z][0][:].bitcast(FP8X4),
+                    lhsT_scale=wq[z][1][:],
+                    rhs=xq[z][0].bitcast(FP8X4),
+                    rhs_scale=xq[z][1],
                     start=(z == 0),
                     stop=(z == PASSES - 1),
                 )
-            y = held.tile([P, SLICE], F32, name=f"y{s}", align_bytes=64)
-            nc.scalar.activation(y[:], acc[:], TANH)
-            nc.vector.tensor_tensor(moved[:, cols], y[:], new_t[:, cols], MULT)
-            for after, a, b in SCATTERS:
-                if after == s:
-                    nc.vector.tensor_tensor(
-                        mem_t[:].indirect(slot_t[:, a // LIST : b // LIST]), moved[:, a:b], kept[:, a:b], ADD
-                    )
+            nc.scalar.activation(y[:, a:b], acc[:], TANH)
+            if s == 0:
+                move(a, b)
+        move(SLICES[0][1], S)
         nc.sync.dma_start(out, mem_t[:])

@@ -21,8 +21,10 @@ P = 128
 PACK = 4
 PASSES = K // (P * PACK)
 LIST = 16
-SLICES = [(0, 128), (128, 256), (256, 512)]
-LOADS = [[(0, 1024, 448)], [(0, 1024, 448)], [(0, 512, 512), (512, 512, 512)], [(0, 512, 512), (512, 512, 256)]]
+HALF = S // 2
+LATE_FIRST = (1, 0)
+SLICES = [(0, 128), (128, 384), (384, 512)]
+LOADS = [[(0, 1024, 448)], [(0, 512, 512), (512, 512, 256)], [(0, 512, 512), (512, 512, 512)], [(0, 512, 512), (512, 512, 256)]]
 
 
 def tile_picked_ema_tanh_e_kernel(tc, xT, mem, w1, old, new, offs, slot, out):
@@ -59,9 +61,9 @@ def tile_picked_ema_tanh_e_kernel(tc, xT, mem, w1, old, new, offs, slot, out):
             for c in range(len(LOADS[q])):
                 if (q, c) != (0, 0):
                     load_x(q, c)
-        w_raw = []
-        for z in range(PASSES):
-            w_raw.append(held.tile([P, PACK, M], F32, name=f"w_raw{z}", tag=f"w_raw{z}", align_bytes=64))
+        w_raw = {}
+        for z in LATE_FIRST:
+            w_raw[z] = held.tile([P, PACK, M], F32, name=f"w_raw{z}", tag=f"w_raw{z}", align_bytes=64)
             nc.sync.dma_start(w_raw[z][:], w_rows[z])
         nc.sync.dma_start(new_t[:], new)
 
@@ -101,48 +103,50 @@ def tile_picked_ema_tanh_e_kernel(tc, xT, mem, w1, old, new, offs, slot, out):
             words = picked[:].bitcast(I32).rearrange("p (j u) -> p j u", u=2)
             nc.vector.tensor_copy(words, halves[:].bitcast(I32).rearrange("p u j -> p j u"))
 
-        def quantize(src, n, name, tag):
-            codes = held.tile([P, n], U32, name=name + "_codes", tag=tag, align_bytes=64)
+        def weave_scalar(picked, halves):
+            words = picked.bitcast(U32).rearrange("p (j u) -> p j u", u=2)
+            nc.scalar.copy(words, halves[:].rearrange("p u j -> p j u"))
+
+        def quantize(src, n, name):
+            codes = held.tile([P, n], U32, name=name + "_codes", align_bytes=64)
             scales = held.tile([P, n], U8, name=name + "_scales", align_bytes=64)
-            nc.vector.quantize_mx(out=codes[:].bitcast(FP8X4), scales=scales[:], in_=src[:])
+            nc.vector.quantize_mx(out=codes[:].bitcast(FP8X4), scales=scales[:], in_=src)
             return codes, scales
 
-        picked0 = held.tile([P, PACK * S], BF16, name="picked0", align_bytes=64)
         halves1 = [held.tile([P, 2, b - a], U32, name=f"halves1_{a}", align_bytes=64) for a, b in SLICES]
-        halves0 = held.tile([P, 2, S], U32, name="halves0", align_bytes=64)
-        cast(0)
-        gather(0, halves0[:, 0, :], 0, S)
-        cast(1)
-        gather(1, halves0[:, 1, :], 0, S)
-        weave(picked0, halves0)
+        halves0 = [held.tile([P, 2, HALF], U32, name=f"halves0_{h}", align_bytes=64) for h in range(2)]
+        picked0 = [held.tile([P, PACK * HALF], BF16, name=f"picked0_{h}", align_bytes=64) for h in range(2)]
+        for q in range(2):
+            cast(q)
+            for h in range(2):
+                gather(q, halves0[h][:, q, :], h * HALF, HALF)
+        for h in range(2):
+            weave(picked0[h], halves0[h])
+        x0_codes = held.tile([P, S], U32, name="x0_codes", align_bytes=64)
+        x0_scales = held.tile([P, S], U8, name="x0_scales", align_bytes=64)
+        for h in range(2):
+            cols = slice(h * HALF, (h + 1) * HALF)
+            nc.vector.quantize_mx(out=x0_codes[:, cols].bitcast(FP8X4), scales=x0_scales[:, cols], in_=picked0[h][:])
         cast(2)
-        x0 = quantize(picked0, S, "x0", "x0_codes")
         for s, (a, b) in enumerate(SLICES):
             gather(2, halves1[s][:, 0, :], a, b - a)
         cast(3)
 
-        w_grouped = []
-        for z in range(PASSES):
-            w_grouped.append(held.tile([P, M * PACK], BF16, name=f"w_grouped{z}", tag=f"w_grouped{z}", align_bytes=64))
+        w_grouped = {}
+        for z in LATE_FIRST:
+            w_grouped[z] = held.tile([P, M * PACK], BF16, name=f"w_grouped{z}", align_bytes=64)
             dst = w_grouped[z][:].rearrange("p (c i j) -> p c j i", i=4, j=PACK)
             nc.scalar.copy(dst, w_raw[z][:].rearrange("p j (c i) -> p c j i", i=4))
 
         for s, (a, b) in enumerate(SLICES):
             gather(3, halves1[s][:, 1, :], a, b - a)
 
-        def woven(s, tag):
-            a, b = SLICES[s]
-            picked = held.tile([P, PACK * (b - a)], BF16, name=f"picked1_{s}", tag=tag, align_bytes=64)
-            weave(picked, halves1[s])
-            return picked
-
-        first = woven(0, "picked1_0")
-        wq = [quantize(w_grouped[0], M, "w0", "w0_codes")]
-        x1 = [quantize(first, SLICES[0][1], "x1_0", "w_grouped0")]
-        wq.append(quantize(w_grouped[1], M, "w1", "w1_codes"))
-        rest = [woven(1, "w_grouped1"), woven(2, "w_raw1")]
-        for s in (1, 2):
-            x1.append(quantize(rest[s - 1], SLICES[s][1] - SLICES[s][0], f"x1_{s}", f"x1_{s}_codes"))
+        wq = {z: quantize(w_grouped[z][:], M, f"w{z}") for z in LATE_FIRST}
+        picked1 = held.tile([P, PACK * S], BF16, name="picked1", tag="w_raw0", align_bytes=64)
+        x1 = []
+        for s, (a, b) in enumerate(SLICES):
+            weave_scalar(picked1[:, PACK * a : PACK * b], halves1[s])
+            x1.append(quantize(picked1[:, PACK * a : PACK * b], b - a, f"x1_{s}"))
 
         y = held.tile([P, S], F32, name="y", align_bytes=64)
 
@@ -153,16 +157,16 @@ def tile_picked_ema_tanh_e_kernel(tc, xT, mem, w1, old, new, offs, slot, out):
 
         for s, (a, b) in enumerate(SLICES):
             acc = sums.tile([P, b - a], F32, name=f"acc{s}")
-            xq = [(x0[0][:, a:b], x0[1][:, a:b]), (x1[s][0][:], x1[s][1][:])]
-            for z in range(PASSES):
+            xq = [(x0_codes[:, a:b], x0_scales[:, a:b]), (x1[s][0][:], x1[s][1][:])]
+            for z in LATE_FIRST:
                 nc.tensor.matmul_mx(
                     out=acc[:],
                     lhsT=wq[z][0][:].bitcast(FP8X4),
                     lhsT_scale=wq[z][1][:],
                     rhs=xq[z][0].bitcast(FP8X4),
                     rhs_scale=xq[z][1],
-                    start=(z == 0),
-                    stop=(z == PASSES - 1),
+                    start=(z == LATE_FIRST[0]),
+                    stop=(z == LATE_FIRST[-1]),
                 )
             nc.scalar.activation(y[:, a:b], acc[:], TANH)
             if s == 0:

@@ -8,7 +8,6 @@ FLOPS = 2 * K * M * S
 
 F32 = mybir.dt.float32
 BF16 = mybir.dt.bfloat16
-I32 = mybir.dt.int32
 U32 = mybir.dt.uint32
 U16 = mybir.dt.uint16
 U8 = mybir.dt.uint8
@@ -16,160 +15,174 @@ FP8X4 = mybir.dt.float8_e4m3fn_x4
 MULT = mybir.AluOpType.mult
 ADD = mybir.AluOpType.add
 TANH = mybir.ActivationFunctionType.Tanh
+COPY = mybir.ActivationFunctionType.Copy
 
 P = 128
 PACK = 4
 PASSES = K // (P * PACK)
 LIST = 16
+SLICE = 128
 HALF = S // 2
-LATE_FIRST = (1, 0)
-SLICES = [(0, 128), (128, 384), (384, 512)]
-LOADS = [[(0, 1024, 448)], [(0, 512, 512), (512, 512, 256)], [(0, 512, 512), (512, 512, 512)], [(0, 512, 512), (512, 512, 256)]]
+RUN = 4
 
 
 def tile_picked_ema_tanh_e_kernel(tc, xT, mem, w1, old, new, offs, slot, out):
     nc = tc.nc
     with ExitStack() as ctx:
         held = ctx.enter_context(tc.tile_pool(name="held", bufs=1))
-        sums = ctx.enter_context(tc.psum_pool(name="sums", bufs=1))
-        turns = ctx.enter_context(tc.psum_pool(name="turns", bufs=4))
+        banks = ctx.enter_context(tc.psum_pool(name="banks", bufs=1))
 
         offs_t = held.tile([P, S // LIST], U16, name="offs_t")
         slot_t = held.tile([P, S // LIST], U16, name="slot_t")
         mem_t = held.tile([P, U], F32, name="mem_t", align_bytes=64)
         old_col = held.tile([P, PACK], F32, name="old_col")
-        new_t = held.tile([P, S], F32, name="new_t", align_bytes=64)
-        warm = held.tile([P, 8], F32, name="warm")
+        new_col = held.tile([P, PACK], F32, name="new_col")
         ident = held.tile([P, P], F32, name="ident", align_bytes=64)
 
-        x_rows = xT.rearrange("(z p u e) t -> z u p e t", z=PASSES, p=P, u=2, e=2)
-        w_rows = w1.rearrange("(z p j) m -> z p j m", z=PASSES, p=P, j=PACK)
+        x_rows = xT.rearrange("(z p t) n -> z t p n", z=PASSES, p=P, t=PACK)
+        w_rows = w1.rearrange("(z p t) m -> z p t m", z=PASSES, p=P, t=PACK)
+        plane = {}
+        w_raw = {}
 
-        raw = {}
+        def load_plane(z, t):
+            plane[z, t] = held.tile([P, T], F32, name=f"plane{z}{t}", align_bytes=64)
+            nc.sync.dma_start(plane[z, t][:], x_rows[z, t])
 
-        def load_x(q, c):
-            t0, n, unused = LOADS[q][c]
-            raw[q, c] = held.tile([P, 2, n], F32, name=f"raw{q}_{c}", align_bytes=64)
-            nc.sync.dma_start(raw[q, c][:], x_rows[q // 2, q % 2][:, :, t0 : t0 + n])
+        def load_w(z):
+            w_raw[z] = held.tile([P, PACK, M], F32, name=f"w_raw{z}", align_bytes=64)
+            nc.sync.dma_start(w_raw[z][:], w_rows[z])
 
         nc.scalar.dma_start(old_col[:], old[0:1, :].rearrange("o (p c) -> (o p) c", c=PACK))
         nc.sync.dma_start(mem_t[:], mem)
         nc.sync.dma_start(slot_t[:], slot)
-        load_x(0, 0)
+        load_plane(0, 0)
         nc.sync.dma_start(offs_t[:], offs)
-        for q in range(2 * PASSES):
-            for c in range(len(LOADS[q])):
-                if (q, c) != (0, 0):
-                    load_x(q, c)
-        w_raw = {}
-        for z in LATE_FIRST:
-            w_raw[z] = held.tile([P, PACK, M], F32, name=f"w_raw{z}", tag=f"w_raw{z}", align_bytes=64)
-            nc.sync.dma_start(w_raw[z][:], w_rows[z])
-        nc.sync.dma_start(new_t[:], new)
+        for t in range(1, PACK):
+            load_plane(0, t)
+        nc.sync.dma_start(new_col[:], new[0:1, :].rearrange("o (p c) -> (o p) c", c=PACK))
+        load_w(0)
+        for t in range(PACK - 1):
+            load_plane(1, t)
+        load_w(1)
+        load_plane(1, PACK - 1)
 
-        nc.gpsimd.memset(warm[:], 0.0)
-        nc.scalar.activation(warm[:, 0:1], warm[:, 1:2], TANH)
         make_identity(nc, ident[:])
 
-        old_ps = turns.tile([P, PACK, P], F32, name="old_ps", tag="turn")
-        for c in range(PACK):
-            nc.tensor.transpose(old_ps[:, c, :], old_col[:, c : c + 1].to_broadcast([P, P]), ident[:])
+        def spread(col, name):
+            bank = banks.tile([P, PACK, P], F32, name=name)
+            for c in range(PACK):
+                nc.tensor.transpose(bank[:, c, :], col[:, c : c + 1].to_broadcast([P, P]), ident[:])
+            return bank[:].rearrange("p c n -> p n c")
+
+        def by_four(ap):
+            return ap.rearrange("p (n c) -> p n c", c=PACK)
+
+        old_all = spread(old_col, "old_all")
+        new_all = spread(new_col, "new_all")
         found = held.tile([P, S], F32, name="found", align_bytes=64)
         nc.vector.tensor_copy(found[:], mem_t[:].indirect(slot_t[:]))
         kept = held.tile([P, S], F32, name="kept", align_bytes=64)
-        nc.vector.tensor_tensor(
-            kept[:].rearrange("p (n c) -> p n c", c=PACK),
-            found[:].rearrange("p (n c) -> p n c", c=PACK),
-            old_ps[:].rearrange("p c n -> p n c"),
-            MULT,
-        )
+        nc.vector.tensor_tensor(by_four(kept[:]), by_four(found[:]), old_all, MULT)
 
-        pairs = [held.tile([P, 2 * T], BF16, name=f"pairs{q}", align_bytes=64) for q in range(2 * PASSES)]
+        def entries(lst, a, b):
+            return lst[:, a // LIST : b // LIST]
 
-        def cast(q):
-            for c, (t0, n, ns) in enumerate(LOADS[q]):
-                src = raw[q, c][:].rearrange("p e t -> p t e")
-                dst = pairs[q][:, 2 * t0 : 2 * (t0 + n)].rearrange("p (t e) -> p t e", e=2)
-                if ns > 0:
-                    nc.scalar.copy(dst[:, 0:ns, :], src[:, 0:ns, :])
-                if ns < n:
-                    nc.vector.tensor_copy(dst[:, ns:n, :], src[:, ns:n, :])
+        def interleaved(dst, src):
+            return (
+                dst.rearrange("p (c i t) -> p c t i", i=RUN, t=PACK),
+                src.rearrange("p t (c i) -> p c t i", i=RUN),
+            )
 
-        def gather(q, target, j0, n):
-            window = pairs[q][:].bitcast(U32)
-            nc.vector.tensor_copy(target, window.indirect(offs_t[:, j0 // LIST : (j0 + n) // LIST]))
+        def quantize(codes, scales, src):
+            nc.vector.quantize_mx(out=codes.bitcast(FP8X4), scales=scales, in_=src)
 
-        def weave(picked, halves):
-            words = picked[:].bitcast(I32).rearrange("p (j u) -> p j u", u=2)
-            nc.vector.tensor_copy(words, halves[:].bitcast(I32).rearrange("p u j -> p j u"))
+        front = [held.tile([P, PACK * HALF], BF16, name=f"front{z}", align_bytes=64) for z in range(PASSES)]
+        back = [held.tile([P, PACK * HALF], BF16, name=f"back{z}", align_bytes=64) for z in range(PASSES)]
+        rows = [held.tile([P, PACK, HALF], BF16, name=f"rows{z}", align_bytes=64) for z in range(PASSES)]
+        x_codes = [held.tile([P, S], U32, name=f"x_codes{z}", align_bytes=64) for z in range(PASSES)]
+        x_scales = [held.tile([P, S], U8, name=f"x_scales{z}", align_bytes=64) for z in range(PASSES)]
+        w_grouped = [held.tile([P, PACK * M], BF16, name=f"w_grouped{z}", align_bytes=64) for z in range(PASSES)]
+        w_codes = [held.tile([P, M], U32, name=f"w_codes{z}", align_bytes=64) for z in range(PASSES)]
+        w_scales = [held.tile([P, M], U8, name=f"w_scales{z}", align_bytes=64) for z in range(PASSES)]
+        slices = [(a, a + SLICE) for a in range(0, S, SLICE)]
+        acc = [banks.tile([P, SLICE], F32, name=f"acc{a}") for a, b in slices]
 
-        def weave_scalar(picked, halves):
-            words = picked.bitcast(U32).rearrange("p (j u) -> p j u", u=2)
-            nc.scalar.copy(words, halves[:].rearrange("p u j -> p j u"))
+        def gather_front(z, t, a, b):
+            dst = front[z][:].rearrange("p (j t) -> p j t", t=PACK)[:, a:b, t]
+            nc.vector.tensor_copy(dst, plane[z, t][:].indirect(entries(offs_t, a, b)))
 
-        def quantize(src, n, name):
-            codes = held.tile([P, n], U32, name=name + "_codes", align_bytes=64)
-            scales = held.tile([P, n], U8, name=name + "_scales", align_bytes=64)
-            nc.vector.quantize_mx(out=codes[:].bitcast(FP8X4), scales=scales[:], in_=src)
-            return codes, scales
+        def gather_rows(z, t):
+            nc.scalar.activation(rows[z][:, t, :], plane[z, t][:].indirect(entries(offs_t, HALF, S)), COPY)
 
-        halves1 = [held.tile([P, 2, b - a], U32, name=f"halves1_{a}", align_bytes=64) for a, b in SLICES]
-        halves0 = [held.tile([P, 2, HALF], U32, name=f"halves0_{h}", align_bytes=64) for h in range(2)]
-        picked0 = [held.tile([P, PACK * HALF], BF16, name=f"picked0_{h}", align_bytes=64) for h in range(2)]
-        for q in range(2):
-            cast(q)
-            for h in range(2):
-                gather(q, halves0[h][:, q, :], h * HALF, HALF)
-        for h in range(2):
-            weave(picked0[h], halves0[h])
-        x0_codes = held.tile([P, S], U32, name="x0_codes", align_bytes=64)
-        x0_scales = held.tile([P, S], U8, name="x0_scales", align_bytes=64)
-        for h in range(2):
-            cols = slice(h * HALF, (h + 1) * HALF)
-            nc.vector.quantize_mx(out=x0_codes[:, cols].bitcast(FP8X4), scales=x0_scales[:, cols], in_=picked0[h][:])
-        cast(2)
-        for s, (a, b) in enumerate(SLICES):
-            gather(2, halves1[s][:, 0, :], a, b - a)
-        cast(3)
+        def back_views(z, a, b):
+            return interleaved(back[z][:, PACK * (a - HALF) : PACK * (b - HALF)], rows[z][:, :, a - HALF : b - HALF])
 
-        w_grouped = {}
-        for z in LATE_FIRST:
-            w_grouped[z] = held.tile([P, M * PACK], BF16, name=f"w_grouped{z}", align_bytes=64)
-            dst = w_grouped[z][:].rearrange("p (c i j) -> p c j i", i=4, j=PACK)
-            nc.scalar.copy(dst, w_raw[z][:].rearrange("p j (c i) -> p c j i", i=4))
+        def quantize_x(z, a, b):
+            if a < HALF:
+                src = front[z][:, PACK * a : PACK * b]
+            else:
+                src = back[z][:, PACK * (a - HALF) : PACK * (b - HALF)]
+            quantize(x_codes[z][:, a:b], x_scales[z][:, a:b], src)
 
-        for s, (a, b) in enumerate(SLICES):
-            gather(3, halves1[s][:, 1, :], a, b - a)
+        def multiply(z, s):
+            a, b = slices[s]
+            nc.tensor.matmul_mx(
+                out=acc[s][:],
+                lhsT=w_codes[z][:].bitcast(FP8X4),
+                lhsT_scale=w_scales[z][:],
+                rhs=x_codes[z][:, a:b].bitcast(FP8X4),
+                rhs_scale=x_scales[z][:, a:b],
+                start=(z == 0),
+                stop=(z == PASSES - 1),
+            )
 
-        wq = {z: quantize(w_grouped[z][:], M, f"w{z}") for z in LATE_FIRST}
-        picked1 = held.tile([P, PACK * S], BF16, name="picked1", tag="w_raw0", align_bytes=64)
-        x1 = []
-        for s, (a, b) in enumerate(SLICES):
-            weave_scalar(picked1[:, PACK * a : PACK * b], halves1[s])
-            x1.append(quantize(picked1[:, PACK * a : PACK * b], b - a, f"x1_{s}"))
+        def prepare_w(z):
+            nc.scalar.copy(*interleaved(w_grouped[z][:], w_raw[z][:]))
+            quantize(w_codes[z][:], w_scales[z][:], w_grouped[z][:])
+
+        for t in range(PACK):
+            gather_front(0, t, 0, HALF)
+            gather_rows(0, t)
+        quantize_x(0, 0, HALF)
+        nc.vector.tensor_copy(*back_views(0, HALF, S))
+        prepare_w(0)
+        quantize_x(0, HALF, S)
+        for s in range(len(slices)):
+            multiply(0, s)
+
+        last = PACK - 1
+        for t in range(last):
+            gather_front(1, t, 0, HALF)
+            gather_rows(1, t)
+        prepare_w(1)
 
         y = held.tile([P, S], F32, name="y", align_bytes=64)
+        moved = held.tile([P, S], F32, name="moved", align_bytes=64)
 
-        def move(a, b):
-            moved = held.tile([P, b - a], F32, name=f"moved{a}", align_bytes=64)
-            nc.vector.tensor_tensor(moved[:], y[:, a:b], new_t[:, a:b], MULT)
-            nc.vector.tensor_tensor(mem_t[:].indirect(slot_t[:, a // LIST : b // LIST]), moved[:], kept[:, a:b], ADD)
+        def finish(s):
+            a, b = slices[s]
+            quantize_x(1, a, b)
+            multiply(1, s)
+            nc.scalar.activation(y[:, a:b], acc[s][:], TANH)
 
-        for s, (a, b) in enumerate(SLICES):
-            acc = sums.tile([P, b - a], F32, name=f"acc{s}")
-            xq = [(x0_codes[:, a:b], x0_scales[:, a:b]), (x1[s][0][:], x1[s][1][:])]
-            for z in LATE_FIRST:
-                nc.tensor.matmul_mx(
-                    out=acc[:],
-                    lhsT=wq[z][0][:].bitcast(FP8X4),
-                    lhsT_scale=wq[z][1][:],
-                    rhs=xq[z][0].bitcast(FP8X4),
-                    rhs_scale=xq[z][1],
-                    start=(z == LATE_FIRST[0]),
-                    stop=(z == LATE_FIRST[-1]),
-                )
-            nc.scalar.activation(y[:, a:b], acc[:], TANH)
-            if s == 0:
-                move(a, b)
-        move(SLICES[0][1], S)
+        def weigh(a, b):
+            nc.vector.tensor_tensor(by_four(moved[:, a:b]), by_four(y[:, a:b]), new_all[:, a // PACK : b // PACK, :], MULT)
+
+        def put(a, b):
+            nc.vector.tensor_tensor(mem_t[:].indirect(entries(slot_t, a, b)), moved[:, a:b], kept[:, a:b], ADD)
+
+        gather_rows(1, last)
+        gather_front(1, last, *slices[0])
+        gather_front(1, last, *slices[1])
+        nc.scalar.copy(*back_views(1, *slices[3]))
+        finish(0)
+        finish(1)
+        nc.vector.tensor_copy(*back_views(1, *slices[2]))
+        finish(3)
+        finish(2)
+        weigh(*slices[0])
+        weigh(*slices[1])
+        put(*slices[0])
+        weigh(HALF, S)
+        put(SLICE, S)
         nc.sync.dma_start(out, mem_t[:])

@@ -22,6 +22,7 @@ PACK = 4
 PASSES = K // (P * PACK)
 LIST = 16
 SLICE = 128
+SLICES = S // SLICE
 HALF = S // 2
 RUN = 4
 
@@ -35,8 +36,7 @@ def tile_picked_ema_tanh_e_kernel(tc, xT, mem, w1, old, new, offs, slot, out):
         offs_t = held.tile([P, S // LIST], U16, name="offs_t")
         slot_t = held.tile([P, S // LIST], U16, name="slot_t")
         mem_t = held.tile([P, U], F32, name="mem_t", align_bytes=64)
-        old_col = held.tile([P, PACK], F32, name="old_col")
-        new_col = held.tile([P, PACK], F32, name="new_col")
+        weights = held.tile([P, P], F32, name="weights", align_bytes=64)
         ident = held.tile([P, P], F32, name="ident", align_bytes=64)
 
         x_rows = xT.rearrange("(z p t) n -> z t p n", z=PASSES, p=P, t=PACK)
@@ -52,14 +52,15 @@ def tile_picked_ema_tanh_e_kernel(tc, xT, mem, w1, old, new, offs, slot, out):
             w_raw[z] = held.tile([P, PACK, M], F32, name=f"w_raw{z}", align_bytes=64)
             nc.sync.dma_start(w_raw[z][:], w_rows[z])
 
-        nc.scalar.dma_start(old_col[:], old[0:1, :].rearrange("o (p c) -> (o p) c", c=PACK))
+        nc.gpsimd.memset(weights[:], 0.0)
+        for r, vec in enumerate((old, new)):
+            nc.scalar.dma_start(weights[r * SLICES : (r + 1) * SLICES, :], vec[0:1, :].rearrange("o (c n) -> (o c) n", n=SLICE))
         nc.sync.dma_start(mem_t[:], mem)
         nc.sync.dma_start(slot_t[:], slot)
         load_plane(0, 0)
         nc.sync.dma_start(offs_t[:], offs)
         for t in range(1, PACK):
             load_plane(0, t)
-        nc.sync.dma_start(new_col[:], new[0:1, :].rearrange("o (p c) -> (o p) c", c=PACK))
         load_w(0)
         for t in range(PACK - 1):
             load_plane(1, t)
@@ -68,21 +69,24 @@ def tile_picked_ema_tanh_e_kernel(tc, xT, mem, w1, old, new, offs, slot, out):
 
         make_identity(nc, ident[:])
 
-        def spread(col, name):
-            bank = banks.tile([P, PACK, P], F32, name=name)
-            for c in range(PACK):
-                nc.tensor.transpose(bank[:, c, :], col[:, c : c + 1].to_broadcast([P, P]), ident[:])
-            return bank[:].rearrange("p c n -> p n c")
+        turned = banks.tile([P, P], F32, name="turned")
+        nc.tensor.transpose(turned[:], weights[:], ident[:])
+        columns = held.tile([P, 2 * SLICES], F32, name="columns")
+        nc.scalar.copy(columns[:], turned[:, 0 : 2 * SLICES])
 
-        def by_four(ap):
-            return ap.rearrange("p (n c) -> p n c", c=PACK)
+        def spread(first, name):
+            bank = banks.tile([P, S], F32, name=name)
+            for c in range(SLICES):
+                column = columns[:, first + c : first + c + 1]
+                nc.tensor.transpose(bank[:, c * SLICE : (c + 1) * SLICE], column.to_broadcast([P, P]), ident[:])
+            return bank
 
-        old_all = spread(old_col, "old_all")
-        new_all = spread(new_col, "new_all")
+        old_all = spread(0, "old_all")
+        new_all = spread(SLICES, "new_all")
         found = held.tile([P, S], F32, name="found", align_bytes=64)
         nc.vector.tensor_copy(found[:], mem_t[:].indirect(slot_t[:]))
         kept = held.tile([P, S], F32, name="kept", align_bytes=64)
-        nc.vector.tensor_tensor(by_four(kept[:]), by_four(found[:]), old_all, MULT)
+        nc.vector.tensor_tensor(kept[:], found[:], old_all[:], MULT)
 
         def entries(lst, a, b):
             return lst[:, a // LIST : b // LIST]
@@ -166,7 +170,7 @@ def tile_picked_ema_tanh_e_kernel(tc, xT, mem, w1, old, new, offs, slot, out):
             nc.scalar.activation(y[:, a:b], acc[s][:], TANH)
 
         def weigh(a, b):
-            nc.vector.tensor_tensor(by_four(moved[:, a:b]), by_four(y[:, a:b]), new_all[:, a // PACK : b // PACK, :], MULT)
+            nc.vector.tensor_tensor(moved[:, a:b], y[:, a:b], new_all[:, a:b], MULT)
 
         def put(a, b):
             nc.vector.tensor_tensor(mem_t[:].indirect(entries(slot_t, a, b)), moved[:, a:b], kept[:, a:b], ADD)

@@ -39,33 +39,36 @@ def tile_picked_ema_tanh_e_kernel(tc, xT, mem, w1, old, new, offs, slot, out):
         weights = held.tile([P, P], F32, name="weights", align_bytes=64)
         ident = held.tile([P, P], F32, name="ident", align_bytes=64)
 
-        x_rows = xT.rearrange("(z p t) n -> z t p n", z=PASSES, p=P, t=PACK)
+        x_rows = xT.rearrange("(z p t) n -> z p t n", z=PASSES, p=P, t=PACK)
         w_rows = w1.rearrange("(z p t) m -> z p t m", z=PASSES, p=P, t=PACK)
         plane = {}
         w_raw = {}
 
-        def load_plane(z, t):
-            plane[z, t] = held.tile([P, T], F32, name=f"plane{z}{t}", align_bytes=64)
-            nc.sync.dma_start(plane[z, t][:], x_rows[z, t])
+        def load_planes(z, t, count):
+            raw = held.tile([P, count, T], F32, name=f"raw{z}{t}", align_bytes=64)
+            nc.sync.dma_start(raw[:], x_rows[z][:, t : t + count, :])
+            for i in range(count):
+                plane[z, t + i] = raw[:, i, :]
 
         def load_w(z):
             w_raw[z] = held.tile([P, PACK, M], F32, name=f"w_raw{z}", align_bytes=64)
             nc.sync.dma_start(w_raw[z][:], w_rows[z])
 
-        nc.gpsimd.memset(weights[:], 0.0)
-        for r, vec in enumerate((old, new)):
-            nc.scalar.dma_start(weights[r * SLICES : (r + 1) * SLICES, :], vec[0:1, :].rearrange("o (c n) -> (o c) n", n=SLICE))
-        nc.sync.dma_start(mem_t[:], mem)
-        nc.sync.dma_start(slot_t[:], slot)
-        load_plane(0, 0)
+        zero = held.tile([P, 1], F32, name="zero")
+        nc.gpsimd.memset(zero[:], 0.0)
+        nc.scalar.activation(weights[:], zero[:].to_broadcast([P, P]), COPY)
+        load_planes(0, 0, 2)
         nc.sync.dma_start(offs_t[:], offs)
-        for t in range(1, PACK):
-            load_plane(0, t)
+        load_planes(0, 2, 2)
+        for r, vec in enumerate((old, new)):
+            nc.sync.dma_start(weights[r * SLICES : (r + 1) * SLICES, :], vec[0:1, :].rearrange("o (c n) -> (o c) n", n=SLICE))
+        nc.sync.dma_start(slot_t[:], slot)
+        nc.sync.dma_start(mem_t[:], mem)
         load_w(0)
         for t in range(PACK - 1):
-            load_plane(1, t)
+            load_planes(1, t, 1)
         load_w(1)
-        load_plane(1, PACK - 1)
+        load_planes(1, PACK - 1, 1)
 
         make_identity(nc, ident[:])
 
@@ -83,10 +86,6 @@ def tile_picked_ema_tanh_e_kernel(tc, xT, mem, w1, old, new, offs, slot, out):
 
         old_all = spread(0, "old_all")
         new_all = spread(SLICES, "new_all")
-        found = held.tile([P, S], F32, name="found", align_bytes=64)
-        nc.vector.tensor_copy(found[:], mem_t[:].indirect(slot_t[:]))
-        kept = held.tile([P, S], F32, name="kept", align_bytes=64)
-        nc.vector.tensor_tensor(kept[:], found[:], old_all[:], MULT)
 
         def entries(lst, a, b):
             return lst[:, a // LIST : b // LIST]
@@ -102,7 +101,7 @@ def tile_picked_ema_tanh_e_kernel(tc, xT, mem, w1, old, new, offs, slot, out):
 
         front = [held.tile([P, PACK * HALF], BF16, name=f"front{z}", align_bytes=64) for z in range(PASSES)]
         back = [held.tile([P, PACK * HALF], BF16, name=f"back{z}", align_bytes=64) for z in range(PASSES)]
-        rows = [held.tile([P, PACK, HALF], BF16, name=f"rows{z}", align_bytes=64) for z in range(PASSES)]
+        rows = [held.tile([P, PACK, HALF], (F32, BF16)[z], name=f"rows{z}", align_bytes=64) for z in range(PASSES)]
         x_codes = [held.tile([P, S], U32, name=f"x_codes{z}", align_bytes=64) for z in range(PASSES)]
         x_scales = [held.tile([P, S], U8, name=f"x_scales{z}", align_bytes=64) for z in range(PASSES)]
         w_grouped = [held.tile([P, PACK * M], BF16, name=f"w_grouped{z}", align_bytes=64) for z in range(PASSES)]
@@ -113,10 +112,10 @@ def tile_picked_ema_tanh_e_kernel(tc, xT, mem, w1, old, new, offs, slot, out):
 
         def gather_front(z, t, a, b):
             dst = front[z][:].rearrange("p (j t) -> p j t", t=PACK)[:, a:b, t]
-            nc.vector.tensor_copy(dst, plane[z, t][:].indirect(entries(offs_t, a, b)))
+            nc.vector.tensor_copy(dst, plane[z, t].indirect(entries(offs_t, a, b)))
 
         def gather_rows(z, t):
-            nc.scalar.activation(rows[z][:, t, :], plane[z, t][:].indirect(entries(offs_t, HALF, S)), COPY)
+            nc.scalar.activation(rows[z][:, t, :], plane[z, t].indirect(entries(offs_t, HALF, S)), COPY)
 
         def back_views(z, a, b):
             return interleaved(back[z][:, PACK * (a - HALF) : PACK * (b - HALF)], rows[z][:, :, a - HALF : b - HALF])
@@ -149,6 +148,10 @@ def tile_picked_ema_tanh_e_kernel(tc, xT, mem, w1, old, new, offs, slot, out):
             gather_rows(0, t)
         quantize_x(0, 0, HALF)
         nc.vector.tensor_copy(*back_views(0, HALF, S))
+        found = held.tile([P, S], F32, name="found", align_bytes=64)
+        nc.scalar.activation(found[:], mem_t[:].indirect(slot_t[:]), COPY)
+        kept = held.tile([P, S], F32, name="kept", align_bytes=64)
+        nc.vector.tensor_tensor(kept[:], found[:], old_all[:], MULT)
         prepare_w(0)
         quantize_x(0, HALF, S)
         for s in range(len(slices)):

@@ -59,16 +59,17 @@ def tile_picked_ema_tanh_e_kernel(tc, xT, mem, w1, old, new, offs, slot, out):
         nc.scalar.activation(weights[:], zero[:].to_broadcast([P, P]), COPY)
         load_planes(0, 0, 2)
         nc.sync.dma_start(offs_t[:], offs)
-        load_planes(0, 2, 2)
+        load_planes(0, 2, 1)
+        load_planes(0, 3, 1)
         for r, vec in enumerate((old, new)):
             nc.sync.dma_start(weights[r * SLICES : (r + 1) * SLICES, :], vec[0:1, :].rearrange("o (c n) -> (o c) n", n=SLICE))
-        nc.sync.dma_start(slot_t[:], slot)
-        nc.sync.dma_start(mem_t[:], mem)
         load_w(0)
         for t in range(PACK - 1):
             load_planes(1, t, 1)
         load_w(1)
         load_planes(1, PACK - 1, 1)
+        nc.sync.dma_start(slot_t[:], slot)
+        nc.sync.dma_start(mem_t[:], mem)
 
         make_identity(nc, ident[:])
 
@@ -148,10 +149,6 @@ def tile_picked_ema_tanh_e_kernel(tc, xT, mem, w1, old, new, offs, slot, out):
             gather_rows(0, t)
         quantize_x(0, 0, HALF)
         nc.vector.tensor_copy(*back_views(0, HALF, S))
-        found = held.tile([P, S], F32, name="found", align_bytes=64)
-        nc.scalar.activation(found[:], mem_t[:].indirect(slot_t[:]), COPY)
-        kept = held.tile([P, S], F32, name="kept", align_bytes=64)
-        nc.vector.tensor_tensor(kept[:], found[:], old_all[:], MULT)
         prepare_w(0)
         quantize_x(0, HALF, S)
         for s in range(len(slices)):
@@ -163,20 +160,14 @@ def tile_picked_ema_tanh_e_kernel(tc, xT, mem, w1, old, new, offs, slot, out):
             gather_rows(1, t)
         prepare_w(1)
 
-        y = held.tile([P, S], F32, name="y", align_bytes=64)
-        moved = held.tile([P, S], F32, name="moved", align_bytes=64)
-
         def finish(s):
-            a, b = slices[s]
-            quantize_x(1, a, b)
+            quantize_x(1, *slices[s])
             multiply(1, s)
-            nc.scalar.activation(y[:, a:b], acc[s][:], TANH)
 
-        def weigh(a, b):
-            nc.vector.tensor_tensor(moved[:, a:b], y[:, a:b], new_all[:, a:b], MULT)
-
-        def put(a, b):
-            nc.vector.tensor_tensor(mem_t[:].indirect(entries(slot_t, a, b)), moved[:, a:b], kept[:, a:b], ADD)
+        def look_up(a, b, tag):
+            found = held.tile([P, b - a], F32, name=f"found{a}", tag=tag, align_bytes=64)
+            nc.scalar.activation(found[:], mem_t[:].indirect(entries(slot_t, a, b)), COPY)
+            return found
 
         gather_rows(1, last)
         gather_front(1, last, *slices[0])
@@ -187,9 +178,29 @@ def tile_picked_ema_tanh_e_kernel(tc, xT, mem, w1, old, new, offs, slot, out):
         nc.vector.tensor_copy(*back_views(1, *slices[2]))
         finish(3)
         finish(2)
+
+        found_first = look_up(0, SLICE, "found_first")
+        found_rest = look_up(SLICE, S, "found_rest")
+        kept_first = held.tile([P, SLICE], F32, name="kept_first", tag="kept", align_bytes=64)
+        nc.vector.tensor_tensor(kept_first[:], found_first[:], old_all[:, 0:SLICE], MULT)
+
+        y = held.tile([P, S], F32, name="y", tag="found_first", align_bytes=64)
+        for s in (0, 1, 3, 2):
+            a, b = slices[s]
+            nc.scalar.activation(y[:, a:b], acc[s][:], TANH)
+
+        moved = held.tile([P, S], F32, name="moved", align_bytes=64)
+
+        def weigh(a, b):
+            nc.vector.tensor_tensor(moved[:, a:b], y[:, a:b], new_all[:, a:b], MULT)
+
         weigh(*slices[0])
         weigh(*slices[1])
-        put(*slices[0])
+        first = held.tile([P, SLICE], F32, name="first", align_bytes=64)
+        nc.vector.tensor_tensor(first[:], moved[:, 0:SLICE], kept_first[:], ADD)
+        nc.scalar.activation(mem_t[:].indirect(entries(slot_t, 0, SLICE)), first[:], COPY)
         weigh(HALF, S)
-        put(SLICE, S)
+        kept_rest = held.tile([P, S - SLICE], F32, name="kept_rest", tag="kept", align_bytes=64)
+        nc.vector.tensor_tensor(kept_rest[:], found_rest[:], old_all[:, SLICE:S], MULT)
+        nc.vector.tensor_tensor(mem_t[:].indirect(entries(slot_t, SLICE, S)), moved[:, SLICE:S], kept_rest[:], ADD)
         nc.sync.dma_start(out, mem_t[:])

@@ -63,12 +63,11 @@ def tile_picked_ema_tanh_e_kernel(tc, xT, mem, w1, old, new, offs, slot, out):
         load_planes(0, 3, 1)
         for r, vec in enumerate((old, new)):
             nc.sync.dma_start(weights[r * SLICES : (r + 1) * SLICES, :], vec[0:1, :].rearrange("o (c n) -> (o c) n", n=SLICE))
-        load_w(0)
-        for t in range(PACK - 1):
-            load_planes(1, t, 1)
-        load_w(1)
-        load_planes(1, PACK - 1, 1)
         nc.sync.dma_start(slot_t[:], slot)
+        for t in range(PACK):
+            load_planes(1, t, 1)
+        for z in range(PASSES):
+            load_w(z)
         nc.sync.dma_start(mem_t[:], mem)
 
         make_identity(nc, ident[:])
@@ -108,8 +107,8 @@ def tile_picked_ema_tanh_e_kernel(tc, xT, mem, w1, old, new, offs, slot, out):
         w_grouped = [held.tile([P, PACK * M], BF16, name=f"w_grouped{z}", align_bytes=64) for z in range(PASSES)]
         w_codes = [held.tile([P, M], U32, name=f"w_codes{z}", align_bytes=64) for z in range(PASSES)]
         w_scales = [held.tile([P, M], U8, name=f"w_scales{z}", align_bytes=64) for z in range(PASSES)]
-        slices = [(a, a + SLICE) for a in range(0, S, SLICE)]
-        acc = [banks.tile([P, SLICE], F32, name=f"acc{a}") for a, b in slices]
+        parts = [(0, SLICE), (SLICE, HALF), (HALF, S)]
+        acc = [banks.tile([P, b - a], F32, name=f"acc{a}") for a, b in parts]
 
         def gather_front(z, t, a, b):
             dst = front[z][:].rearrange("p (j t) -> p j t", t=PACK)[:, a:b, t]
@@ -129,7 +128,7 @@ def tile_picked_ema_tanh_e_kernel(tc, xT, mem, w1, old, new, offs, slot, out):
             quantize(x_codes[z][:, a:b], x_scales[z][:, a:b], src)
 
         def multiply(z, s):
-            a, b = slices[s]
+            a, b = parts[s]
             nc.tensor.matmul_mx(
                 out=acc[s][:],
                 lhsT=w_codes[z][:].bitcast(FP8X4),
@@ -144,63 +143,52 @@ def tile_picked_ema_tanh_e_kernel(tc, xT, mem, w1, old, new, offs, slot, out):
             nc.scalar.copy(*interleaved(w_grouped[z][:], w_raw[z][:]))
             quantize(w_codes[z][:], w_scales[z][:], w_grouped[z][:])
 
-        for t in range(PACK):
-            gather_front(0, t, 0, HALF)
-            gather_rows(0, t)
-        quantize_x(0, 0, HALF)
-        nc.vector.tensor_copy(*back_views(0, HALF, S))
-        prepare_w(0)
-        quantize_x(0, HALF, S)
-        for s in range(len(slices)):
-            multiply(0, s)
+        for z in range(PASSES):
+            for t in range(PACK):
+                gather_front(z, t, 0, HALF)
+                gather_rows(z, t)
+            if z == 0:
+                quantize_x(z, 0, HALF)
+                nc.scalar.copy(*back_views(z, HALF, S))
+            else:
+                nc.vector.tensor_copy(*back_views(z, HALF, S))
+                quantize_x(z, 0, HALF)
+            quantize_x(z, HALF, S)
+        for z in range(PASSES):
+            prepare_w(z)
+            for s in range(len(parts)):
+                multiply(z, s)
 
-        last = PACK - 1
-        for t in range(last):
-            gather_front(1, t, 0, HALF)
-            gather_rows(1, t)
-        prepare_w(1)
-
-        def finish(s):
-            quantize_x(1, *slices[s])
-            multiply(1, s)
-
-        def look_up(a, b, tag):
-            found = held.tile([P, b - a], F32, name=f"found{a}", tag=tag, align_bytes=64)
-            nc.scalar.activation(found[:], mem_t[:].indirect(entries(slot_t, a, b)), COPY)
-            return found
-
-        gather_rows(1, last)
-        gather_front(1, last, *slices[0])
-        gather_front(1, last, *slices[1])
-        nc.scalar.copy(*back_views(1, *slices[3]))
-        finish(0)
-        finish(1)
-        nc.vector.tensor_copy(*back_views(1, *slices[2]))
-        finish(3)
-        finish(2)
-
-        found_first = look_up(0, SLICE, "found_first")
-        found_rest = look_up(SLICE, S, "found_rest")
-        kept_first = held.tile([P, SLICE], F32, name="kept_first", tag="kept", align_bytes=64)
-        nc.vector.tensor_tensor(kept_first[:], found_first[:], old_all[:, 0:SLICE], MULT)
-
-        y = held.tile([P, S], F32, name="y", tag="found_first", align_bytes=64)
-        for s in (0, 1, 3, 2):
-            a, b = slices[s]
-            nc.scalar.activation(y[:, a:b], acc[s][:], TANH)
-
+        found_first = held.tile([P, SLICE], F32, name="found_first", tag="found_first", align_bytes=64)
+        found_rest = held.tile([P, S - SLICE], F32, name="found_rest", align_bytes=64)
+        kept = held.tile([P, S], F32, name="kept", align_bytes=64)
         moved = held.tile([P, S], F32, name="moved", align_bytes=64)
+
+        def window(a, b):
+            return mem_t[:].indirect(entries(slot_t, a, b))
+
+        def keep(a, b, found):
+            nc.vector.tensor_tensor(kept[:, a:b], found, old_all[:, a:b], MULT)
 
         def weigh(a, b):
             nc.vector.tensor_tensor(moved[:, a:b], y[:, a:b], new_all[:, a:b], MULT)
 
-        weigh(*slices[0])
-        weigh(*slices[1])
-        first = held.tile([P, SLICE], F32, name="first", align_bytes=64)
-        nc.vector.tensor_tensor(first[:], moved[:, 0:SLICE], kept_first[:], ADD)
-        nc.scalar.activation(mem_t[:].indirect(entries(slot_t, 0, SLICE)), first[:], COPY)
-        weigh(HALF, S)
-        kept_rest = held.tile([P, S - SLICE], F32, name="kept_rest", tag="kept", align_bytes=64)
-        nc.vector.tensor_tensor(kept_rest[:], found_rest[:], old_all[:, SLICE:S], MULT)
-        nc.vector.tensor_tensor(mem_t[:].indirect(entries(slot_t, SLICE, S)), moved[:, SLICE:S], kept_rest[:], ADD)
+        def put(a, b):
+            nc.vector.tensor_tensor(window(a, b), moved[:, a:b], kept[:, a:b], ADD)
+
+        tail = S - SLICE
+        nc.scalar.activation(found_first[:], window(0, SLICE), COPY)
+        nc.scalar.activation(found_rest[:, 0:HALF], window(SLICE, tail), COPY)
+        nc.vector.tensor_copy(found_rest[:, HALF:tail], window(tail, S))
+        keep(0, SLICE, found_first[:])
+        keep(tail, S, found_rest[:, HALF:tail])
+        keep(SLICE, tail, found_rest[:, 0:HALF])
+        y = held.tile([P, S], F32, name="y", tag="found_first", align_bytes=64)
+        for s, (a, b) in enumerate(parts):
+            nc.scalar.activation(y[:, a:b], acc[s][:], TANH)
+        weigh(*parts[0])
+        weigh(*parts[1])
+        put(*parts[0])
+        weigh(*parts[2])
+        put(SLICE, S)
         nc.sync.dma_start(out, mem_t[:])

@@ -99,9 +99,8 @@ def tile_picked_ema_tanh_e_kernel(tc, xT, mem, w1, old, new, offs, slot, out):
         def quantize(codes, scales, src):
             nc.vector.quantize_mx(out=codes.bitcast(FP8X4), scales=scales, in_=src)
 
-        front = [held.tile([P, PACK * HALF], BF16, name=f"front{z}", align_bytes=64) for z in range(PASSES)]
-        back = [held.tile([P, PACK * HALF], BF16, name=f"back{z}", align_bytes=64) for z in range(PASSES)]
-        rows = [held.tile([P, PACK, HALF], (F32, BF16)[z], name=f"rows{z}", align_bytes=64) for z in range(PASSES)]
+        rows = [held.tile([P, PACK, S], (F32, BF16)[z], name=f"rows{z}", align_bytes=64) for z in range(PASSES)]
+        grouped = [held.tile([P, PACK * S], BF16, name=f"grouped{z}", align_bytes=64) for z in range(PASSES)]
         x_codes = [held.tile([P, S], U32, name=f"x_codes{z}", align_bytes=64) for z in range(PASSES)]
         x_scales = [held.tile([P, S], U8, name=f"x_scales{z}", align_bytes=64) for z in range(PASSES)]
         w_grouped = [held.tile([P, PACK * M], BF16, name=f"w_grouped{z}", align_bytes=64) for z in range(PASSES)]
@@ -110,22 +109,17 @@ def tile_picked_ema_tanh_e_kernel(tc, xT, mem, w1, old, new, offs, slot, out):
         parts = [(0, SLICE), (SLICE, HALF), (HALF, S)]
         acc = [banks.tile([P, b - a], F32, name=f"acc{a}") for a, b in parts]
 
-        def gather_front(z, t, a, b):
-            dst = front[z][:].rearrange("p (j t) -> p j t", t=PACK)[:, a:b, t]
-            nc.vector.tensor_copy(dst, plane[z, t].indirect(entries(offs_t, a, b)))
+        def picked(z, t, a, b):
+            return plane[z, t].indirect(entries(offs_t, a, b))
 
-        def gather_rows(z, t):
-            nc.scalar.activation(rows[z][:, t, :], plane[z, t].indirect(entries(offs_t, HALF, S)), COPY)
+        def gather_rows(z, t, a, b):
+            nc.scalar.activation(rows[z][:, t, a:b], picked(z, t, a, b), COPY)
 
-        def back_views(z, a, b):
-            return interleaved(back[z][:, PACK * (a - HALF) : PACK * (b - HALF)], rows[z][:, :, a - HALF : b - HALF])
+        def interleave_rows(z, a, b):
+            nc.vector.tensor_copy(*interleaved(grouped[z][:, PACK * a : PACK * b], rows[z][:, :, a:b]))
 
         def quantize_x(z, a, b):
-            if a < HALF:
-                src = front[z][:, PACK * a : PACK * b]
-            else:
-                src = back[z][:, PACK * (a - HALF) : PACK * (b - HALF)]
-            quantize(x_codes[z][:, a:b], x_scales[z][:, a:b], src)
+            quantize(x_codes[z][:, a:b], x_scales[z][:, a:b], grouped[z][:, PACK * a : PACK * b])
 
         def multiply(z, s):
             a, b = parts[s]
@@ -143,17 +137,26 @@ def tile_picked_ema_tanh_e_kernel(tc, xT, mem, w1, old, new, offs, slot, out):
             nc.scalar.copy(*interleaved(w_grouped[z][:], w_raw[z][:]))
             quantize(w_codes[z][:], w_scales[z][:], w_grouped[z][:])
 
-        for z in range(PASSES):
-            for t in range(PACK):
-                gather_front(z, t, 0, HALF)
-                gather_rows(z, t)
-            if z == 0:
-                quantize_x(z, 0, HALF)
-                nc.scalar.copy(*back_views(z, HALF, S))
-            else:
-                nc.vector.tensor_copy(*back_views(z, HALF, S))
-                quantize_x(z, 0, HALF)
-            quantize_x(z, HALF, S)
+        for t in range(PACK):
+            nc.vector.tensor_copy(rows[0][:, t, 0:HALF], picked(0, t, 0, HALF))
+            gather_rows(0, t, HALF, S)
+        for a in (0, HALF):
+            interleave_rows(0, a, a + HALF)
+        for a in (0, HALF):
+            quantize_x(0, a, a + HALF)
+
+        first = grouped[1][:, 0 : PACK * SLICE].rearrange("p (j t) -> p j t", t=PACK)
+        for t in range(PACK):
+            nc.vector.tensor_copy(first[:, :, t], picked(1, t, 0, SLICE))
+            if t < PACK - 1:
+                gather_rows(1, t, SLICE, S)
+        gather_rows(1, PACK - 1, SLICE, HALF)
+        gather_rows(1, PACK - 1, HALF, S)
+        interleave_rows(1, SLICE, HALF)
+        quantize_x(1, 0, SLICE)
+        interleave_rows(1, HALF, S)
+        quantize_x(1, SLICE, HALF)
+        quantize_x(1, HALF, S)
         for z in range(PASSES):
             prepare_w(z)
             for s in range(len(parts)):

@@ -63,11 +63,11 @@ def tile_picked_ema_tanh_e_kernel(tc, xT, mem, w1, old, new, offs, slot, out):
         load_planes(0, 3, 1)
         for r, vec in enumerate((old, new)):
             nc.sync.dma_start(weights[r * SLICES : (r + 1) * SLICES, :], vec[0:1, :].rearrange("o (c n) -> (o c) n", n=SLICE))
-        nc.sync.dma_start(slot_t[:], slot)
         for t in range(PACK):
             load_planes(1, t, 1)
         for z in range(PASSES):
             load_w(z)
+        nc.sync.dma_start(slot_t[:], slot)
         nc.sync.dma_start(mem_t[:], mem)
 
         make_identity(nc, ident[:])
@@ -184,14 +184,11 @@ def tile_picked_ema_tanh_e_kernel(tc, xT, mem, w1, old, new, offs, slot, out):
         nc.scalar.activation(found_rest[:, 0:HALF], window(SLICE, tail), COPY)
         nc.vector.tensor_copy(found_rest[:, HALF:tail], window(tail, S))
         keep(0, SLICE, found_first[:])
-        keep(tail, S, found_rest[:, HALF:tail])
-        keep(SLICE, tail, found_rest[:, 0:HALF])
+        keep(SLICE, S, found_rest[:])
         y = held.tile([P, S], F32, name="y", tag="found_first", align_bytes=64)
         for s, (a, b) in enumerate(parts):
             nc.scalar.activation(y[:, a:b], acc[s][:], TANH)
-        weigh(*parts[0])
-        weigh(*parts[1])
-        put(*parts[0])
-        weigh(*parts[2])
-        put(SLICE, S)
+        weigh(0, HALF)
+        weigh(HALF, S)
+        put(0, S)
         nc.sync.dma_start(out, mem_t[:])

@@ -59,8 +59,7 @@ def tile_picked_ema_tanh_e_kernel(tc, xT, mem, w1, old, new, offs, slot, out):
         nc.scalar.activation(weights[:], zero[:].to_broadcast([P, P]), COPY)
         load_planes(0, 0, 2)
         nc.sync.dma_start(offs_t[:], offs)
-        load_planes(0, 2, 1)
-        load_planes(0, 3, 1)
+        load_planes(0, 2, 2)
         for r, vec in enumerate((old, new)):
             nc.sync.dma_start(weights[r * SLICES : (r + 1) * SLICES, :], vec[0:1, :].rearrange("o (c n) -> (o c) n", n=SLICE))
         for t in range(PACK):

@@ -25,6 +25,8 @@ SLICE = 128
 SLICES = S // SLICE
 HALF = S // 2
 RUN = 4
+PLAIN = 384
+LEAD = 448
 
 
 def tile_picked_ema_tanh_e_kernel(tc, xT, mem, w1, old, new, offs, slot, out):
@@ -51,17 +53,18 @@ def tile_picked_ema_tanh_e_kernel(tc, xT, mem, w1, old, new, offs, slot, out):
                 plane[z, t + i] = raw[:, i, :]
 
         def load_w(z):
-            w_raw[z] = held.tile([P, PACK, M], F32, name=f"w_raw{z}", align_bytes=64)
+            w_raw[z] = held.tile([P, PACK, M], F32, name=f"w_raw{z}", tag=f"w_raw{z}", align_bytes=64)
             nc.sync.dma_start(w_raw[z][:], w_rows[z])
 
         zero = held.tile([P, 1], F32, name="zero")
         nc.gpsimd.memset(zero[:], 0.0)
-        nc.scalar.activation(weights[:], zero[:].to_broadcast([P, P]), COPY)
+        nc.gpsimd.memset(weights[0 : P // 2, :], 0.0)
+        nc.scalar.activation(weights[P // 2 :, :], zero[P // 2 :, :].to_broadcast([P // 2, P]), COPY)
         load_planes(0, 0, 2)
         nc.sync.dma_start(offs_t[:], offs)
-        load_planes(0, 2, 2)
         for r, vec in enumerate((old, new)):
             nc.sync.dma_start(weights[r * SLICES : (r + 1) * SLICES, :], vec[0:1, :].rearrange("o (c n) -> (o c) n", n=SLICE))
+        load_planes(0, 2, 2)
         for t in range(PACK):
             load_planes(1, t, 1)
         for z in range(PASSES):
@@ -76,15 +79,20 @@ def tile_picked_ema_tanh_e_kernel(tc, xT, mem, w1, old, new, offs, slot, out):
         columns = held.tile([P, 2 * SLICES], F32, name="columns")
         nc.scalar.copy(columns[:], turned[:, 0 : 2 * SLICES])
 
-        def spread(first, name):
+        def spread(first, count, name):
             bank = banks.tile([P, S], F32, name=name)
-            for c in range(SLICES):
+            for c in range(count):
                 column = columns[:, first + c : first + c + 1]
                 nc.tensor.transpose(bank[:, c * SLICE : (c + 1) * SLICE], column.to_broadcast([P, P]), ident[:])
             return bank
 
-        old_all = spread(0, "old_all")
-        new_all = spread(SLICES, "new_all")
+        old_last = spread(SLICES - 1, 1, "old_last")
+        old_t = {}
+        for a, b in ((LEAD, S), (PLAIN, LEAD)):
+            old_t[a] = held.tile([P, b - a], F32, name=f"old{a}", tag=f"old{a}", align_bytes=64)
+            nc.vector.tensor_copy(old_t[a][:], old_last[:, a - PLAIN : b - PLAIN])
+        old_all = spread(0, SLICES - 1, "old_all")
+        new_all = spread(SLICES, SLICES, "new_all")
 
         def entries(lst, a, b):
             return lst[:, a // LIST : b // LIST]
@@ -99,13 +107,13 @@ def tile_picked_ema_tanh_e_kernel(tc, xT, mem, w1, old, new, offs, slot, out):
             nc.vector.quantize_mx(out=codes.bitcast(FP8X4), scales=scales, in_=src)
 
         rows = [held.tile([P, PACK, S], (F32, BF16)[z], name=f"rows{z}", align_bytes=64) for z in range(PASSES)]
-        grouped = [held.tile([P, PACK * S], BF16, name=f"grouped{z}", align_bytes=64) for z in range(PASSES)]
-        x_codes = [held.tile([P, S], U32, name=f"x_codes{z}", align_bytes=64) for z in range(PASSES)]
+        grouped = {}
+        x_codes = {}
         x_scales = [held.tile([P, S], U8, name=f"x_scales{z}", align_bytes=64) for z in range(PASSES)]
-        w_grouped = [held.tile([P, PACK * M], BF16, name=f"w_grouped{z}", align_bytes=64) for z in range(PASSES)]
+        w_grouped = [held.tile([P, PACK * M], BF16, name=f"w_grouped{z}", tag=f"w_grouped{z}", align_bytes=64) for z in range(PASSES)]
         w_codes = [held.tile([P, M], U32, name=f"w_codes{z}", align_bytes=64) for z in range(PASSES)]
         w_scales = [held.tile([P, M], U8, name=f"w_scales{z}", align_bytes=64) for z in range(PASSES)]
-        parts = [(0, SLICE), (SLICE, HALF), (HALF, S)]
+        parts = [(0, HALF), (HALF, S)]
         acc = [banks.tile([P, b - a], F32, name=f"acc{a}") for a, b in parts]
 
         def picked(z, t, a, b):
@@ -114,11 +122,20 @@ def tile_picked_ema_tanh_e_kernel(tc, xT, mem, w1, old, new, offs, slot, out):
         def gather_rows(z, t, a, b):
             nc.scalar.activation(rows[z][:, t, a:b], picked(z, t, a, b), COPY)
 
+        def hold_grouped(z, a, b, tag):
+            grouped[z, a, b] = held.tile([P, PACK * (b - a)], BF16, name=f"grouped{z}_{a}", tag=tag, align_bytes=64)[:]
+
         def interleave_rows(z, a, b):
-            nc.vector.tensor_copy(*interleaved(grouped[z][:, PACK * a : PACK * b], rows[z][:, :, a:b]))
+            nc.vector.tensor_copy(*interleaved(grouped[z, a, b], rows[z][:, :, a:b]))
+
+        def hold_codes(z, a, b, tag):
+            tile = held.tile([P, b - a], U32, name=f"x_codes{z}_{a}", tag=tag, align_bytes=64)
+            for c in range(a, b, SLICE):
+                x_codes[z, c, c + SLICE] = tile[:, c - a : c - a + SLICE]
+            x_codes[z, a, b] = tile[:]
 
         def quantize_x(z, a, b):
-            quantize(x_codes[z][:, a:b], x_scales[z][:, a:b], grouped[z][:, PACK * a : PACK * b])
+            quantize(x_codes[z, a, b], x_scales[z][:, a:b], grouped[z, a, b])
 
         def multiply(z, s):
             a, b = parts[s]
@@ -126,7 +143,7 @@ def tile_picked_ema_tanh_e_kernel(tc, xT, mem, w1, old, new, offs, slot, out):
                 out=acc[s][:],
                 lhsT=w_codes[z][:].bitcast(FP8X4),
                 lhsT_scale=w_scales[z][:],
-                rhs=x_codes[z][:, a:b].bitcast(FP8X4),
+                rhs=x_codes[z, a, b].bitcast(FP8X4),
                 rhs_scale=x_scales[z][:, a:b],
                 start=(z == 0),
                 stop=(z == PASSES - 1),
@@ -140,54 +157,60 @@ def tile_picked_ema_tanh_e_kernel(tc, xT, mem, w1, old, new, offs, slot, out):
             nc.vector.tensor_copy(rows[0][:, t, 0:HALF], picked(0, t, 0, HALF))
             gather_rows(0, t, HALF, S)
         for a in (0, HALF):
+            hold_grouped(0, a, a + HALF, f"grouped0_{a}")
             interleave_rows(0, a, a + HALF)
         for a in (0, HALF):
+            hold_codes(0, a, a + HALF, f"codes0_{a}")
             quantize_x(0, a, a + HALF)
 
-        first = grouped[1][:, 0 : PACK * SLICE].rearrange("p (j t) -> p j t", t=PACK)
-        for t in range(PACK):
+        tail = S - SLICE
+        last = PACK - 1
+        hold_grouped(1, 0, HALF, "grouped1_0")
+        hold_grouped(1, HALF, tail, "grouped1_2")
+        first = grouped[1, 0, HALF][:, 0 : PACK * SLICE].rearrange("p (j t) -> p j t", t=PACK)
+        for t in range(last):
             nc.vector.tensor_copy(first[:, :, t], picked(1, t, 0, SLICE))
-            if t < PACK - 1:
-                gather_rows(1, t, SLICE, S)
-        gather_rows(1, PACK - 1, SLICE, HALF)
-        gather_rows(1, PACK - 1, HALF, S)
-        interleave_rows(1, SLICE, HALF)
-        quantize_x(1, 0, SLICE)
-        interleave_rows(1, HALF, S)
-        quantize_x(1, SLICE, HALF)
-        quantize_x(1, HALF, S)
-        for z in range(PASSES):
-            prepare_w(z)
-            for s in range(len(parts)):
-                multiply(z, s)
+            gather_rows(1, t, SLICE, S)
+        nc.vector.tensor_copy(rows[1][:, last, SLICE:HALF], picked(1, last, SLICE, HALF))
+        nc.vector.tensor_copy(first[:, :, last], picked(1, last, 0, SLICE))
+        gather_rows(1, last, HALF, tail)
+        gather_rows(1, last, tail, S)
+        interleave_rows(1, HALF, tail)
+        nc.vector.tensor_copy(*interleaved(grouped[1, 0, HALF][:, PACK * SLICE :], rows[1][:, :, SLICE:HALF]))
+        prepare_w(0)
+        for s in range(len(parts)):
+            multiply(0, s)
+        hold_codes(1, 0, HALF, "w_raw0")
+        quantize_x(1, 0, HALF)
+        hold_grouped(1, tail, S, "w_grouped0")
+        cut = PACK * (LEAD - tail)
+        nc.vector.tensor_copy(*interleaved(grouped[1, tail, S][:, 0:cut], rows[1][:, :, tail:LEAD]))
+        prepare_w(1)
+        nc.scalar.copy(*interleaved(grouped[1, tail, S][:, cut:], rows[1][:, :, LEAD:S]))
+        hold_codes(1, HALF, S, "w_raw1")
+        quantize_x(1, HALF, tail)
+        quantize_x(1, tail, S)
+        for s in range(len(parts)):
+            multiply(1, s)
 
-        found_first = held.tile([P, SLICE], F32, name="found_first", tag="found_first", align_bytes=64)
-        found_rest = held.tile([P, S - SLICE], F32, name="found_rest", align_bytes=64)
+        found = held.tile([P, PLAIN], F32, name="found", align_bytes=64)
         kept = held.tile([P, S], F32, name="kept", align_bytes=64)
         moved = held.tile([P, S], F32, name="moved", align_bytes=64)
 
         def window(a, b):
             return mem_t[:].indirect(entries(slot_t, a, b))
 
-        def keep(a, b, found):
-            nc.vector.tensor_tensor(kept[:, a:b], found, old_all[:, a:b], MULT)
-
         def weigh(a, b):
             nc.vector.tensor_tensor(moved[:, a:b], y[:, a:b], new_all[:, a:b], MULT)
 
-        def put(a, b):
-            nc.vector.tensor_tensor(window(a, b), moved[:, a:b], kept[:, a:b], ADD)
-
-        tail = S - SLICE
-        nc.scalar.activation(found_first[:], window(0, SLICE), COPY)
-        nc.scalar.activation(found_rest[:, 0:HALF], window(SLICE, tail), COPY)
-        nc.vector.tensor_copy(found_rest[:, HALF:tail], window(tail, S))
-        keep(0, SLICE, found_first[:])
-        keep(SLICE, S, found_rest[:])
-        y = held.tile([P, S], F32, name="y", tag="found_first", align_bytes=64)
+        nc.scalar.activation(found[:], window(0, PLAIN), COPY)
+        nc.vector.tensor_tensor(kept[:, LEAD:S], window(LEAD, S), old_t[LEAD][:], MULT)
+        nc.vector.tensor_tensor(kept[:, PLAIN:LEAD], window(PLAIN, LEAD), old_t[PLAIN][:], MULT)
+        nc.vector.tensor_tensor(kept[:, 0:PLAIN], found[:], old_all[:, 0:PLAIN], MULT)
+        y = held.tile([P, S], F32, name="y", tag=f"old{LEAD}", align_bytes=64)
         for s, (a, b) in enumerate(parts):
             nc.scalar.activation(y[:, a:b], acc[s][:], TANH)
         weigh(0, HALF)
         weigh(HALF, S)
-        put(0, S)
+        nc.vector.tensor_tensor(window(0, S), moved[:], kept[:], ADD)
         nc.sync.dma_start(out, mem_t[:])

@@ -25,7 +25,7 @@ SLICE = 128
 SLICES = S // SLICE
 HALF = S // 2
 RUN = 4
-PLAIN = 384
+PLAIN = 256
 LEAD = 448
 
 
@@ -67,10 +67,12 @@ def tile_picked_ema_tanh_e_kernel(tc, xT, mem, w1, old, new, offs, slot, out):
         load_planes(0, 2, 2)
         for t in range(PACK):
             load_planes(1, t, 1)
-        for z in range(PASSES):
-            load_w(z)
         nc.sync.dma_start(slot_t[:], slot)
+        load_w(0)
+        load_w(1)
         nc.sync.dma_start(mem_t[:], mem)
+        old_plain = held.tile([P, PLAIN], F32, name="old_plain", align_bytes=64)
+        nc.sync.dma_start(old_plain[:], old[:, 0:PLAIN])
 
         make_identity(nc, ident[:])
 
@@ -86,12 +88,9 @@ def tile_picked_ema_tanh_e_kernel(tc, xT, mem, w1, old, new, offs, slot, out):
                 nc.tensor.transpose(bank[:, c * SLICE : (c + 1) * SLICE], column.to_broadcast([P, P]), ident[:])
             return bank
 
-        old_last = spread(SLICES - 1, 1, "old_last")
-        old_t = {}
-        for a, b in ((LEAD, S), (PLAIN, LEAD)):
-            old_t[a] = held.tile([P, b - a], F32, name=f"old{a}", tag=f"old{a}", align_bytes=64)
-            nc.vector.tensor_copy(old_t[a][:], old_last[:, a - PLAIN : b - PLAIN])
-        old_all = spread(0, SLICES - 1, "old_all")
+        old_last = spread(SLICES - 2, 2, "old_last")
+        old_fused = held.tile([P, S - PLAIN], F32, name="old_fused", align_bytes=64)
+        nc.vector.tensor_copy(old_fused[:], old_last[:, PLAIN - HALF : S - HALF])
         new_all = spread(SLICES, SLICES, "new_all")
 
         def entries(lst, a, b):
@@ -113,7 +112,7 @@ def tile_picked_ema_tanh_e_kernel(tc, xT, mem, w1, old, new, offs, slot, out):
         w_grouped = [held.tile([P, PACK * M], BF16, name=f"w_grouped{z}", tag=f"w_grouped{z}", align_bytes=64) for z in range(PASSES)]
         w_codes = [held.tile([P, M], U32, name=f"w_codes{z}", align_bytes=64) for z in range(PASSES)]
         w_scales = [held.tile([P, M], U8, name=f"w_scales{z}", align_bytes=64) for z in range(PASSES)]
-        parts = [(0, HALF), (HALF, S)]
+        parts = [(0, HALF), (HALF, S - SLICE), (S - SLICE, S)]
         acc = [banks.tile([P, b - a], F32, name=f"acc{a}") for a, b in parts]
 
         def picked(z, t, a, b):
@@ -194,7 +193,7 @@ def tile_picked_ema_tanh_e_kernel(tc, xT, mem, w1, old, new, offs, slot, out):
             multiply(1, s)
 
         found = held.tile([P, PLAIN], F32, name="found", align_bytes=64)
-        kept = held.tile([P, S], F32, name="kept", align_bytes=64)
+        kept = held.tile([P, S], F32, name="kept", tag="grouped1_2", align_bytes=64)
         moved = held.tile([P, S], F32, name="moved", align_bytes=64)
 
         def window(a, b):
@@ -204,10 +203,9 @@ def tile_picked_ema_tanh_e_kernel(tc, xT, mem, w1, old, new, offs, slot, out):
             nc.vector.tensor_tensor(moved[:, a:b], y[:, a:b], new_all[:, a:b], MULT)
 
         nc.scalar.activation(found[:], window(0, PLAIN), COPY)
-        nc.vector.tensor_tensor(kept[:, LEAD:S], window(LEAD, S), old_t[LEAD][:], MULT)
-        nc.vector.tensor_tensor(kept[:, PLAIN:LEAD], window(PLAIN, LEAD), old_t[PLAIN][:], MULT)
-        nc.vector.tensor_tensor(kept[:, 0:PLAIN], found[:], old_all[:, 0:PLAIN], MULT)
-        y = held.tile([P, S], F32, name="y", tag=f"old{LEAD}", align_bytes=64)
+        nc.vector.tensor_tensor(kept[:, PLAIN:S], window(PLAIN, S), old_fused[:], MULT)
+        nc.gpsimd.tensor_tensor(kept[:, 0:PLAIN], found[:], old_plain[:], MULT)
+        y = held.tile([P, S], F32, name="y", align_bytes=64)
         for s, (a, b) in enumerate(parts):
             nc.scalar.activation(y[:, a:b], acc[s][:], TANH)
         weigh(0, HALF)

@@ -25,7 +25,7 @@ SLICE = 128
 SLICES = S // SLICE
 HALF = S // 2
 RUN = 4
-PLAIN = 256
+PLAIN = 320
 LEAD = 448
 
 
@@ -71,8 +71,6 @@ def tile_picked_ema_tanh_e_kernel(tc, xT, mem, w1, old, new, offs, slot, out):
         load_w(0)
         load_w(1)
         nc.sync.dma_start(mem_t[:], mem)
-        old_plain = held.tile([P, PLAIN], F32, name="old_plain", align_bytes=64)
-        nc.sync.dma_start(old_plain[:], old[:, 0:PLAIN])
 
         make_identity(nc, ident[:])
 
@@ -91,6 +89,7 @@ def tile_picked_ema_tanh_e_kernel(tc, xT, mem, w1, old, new, offs, slot, out):
         old_last = spread(SLICES - 2, 2, "old_last")
         old_fused = held.tile([P, S - PLAIN], F32, name="old_fused", align_bytes=64)
         nc.vector.tensor_copy(old_fused[:], old_last[:, PLAIN - HALF : S - HALF])
+        old_all = spread(0, SLICES - 1, "old_all")
         new_all = spread(SLICES, SLICES, "new_all")
 
         def entries(lst, a, b):
@@ -204,7 +203,7 @@ def tile_picked_ema_tanh_e_kernel(tc, xT, mem, w1, old, new, offs, slot, out):
 
         nc.scalar.activation(found[:], window(0, PLAIN), COPY)
         nc.vector.tensor_tensor(kept[:, PLAIN:S], window(PLAIN, S), old_fused[:], MULT)
-        nc.gpsimd.tensor_tensor(kept[:, 0:PLAIN], found[:], old_plain[:], MULT)
+        nc.vector.tensor_tensor(kept[:, 0:PLAIN], found[:], old_all[:, 0:PLAIN], MULT)
         y = held.tile([P, S], F32, name="y", align_bytes=64)
         for s, (a, b) in enumerate(parts):
             nc.scalar.activation(y[:, a:b], acc[s][:], TANH)

@@ -25,7 +25,7 @@ SLICE = 128
 SLICES = S // SLICE
 HALF = S // 2
 RUN = 4
-PLAIN = 320
+PLAIN = 256
 LEAD = 448
 
 
@@ -89,7 +89,7 @@ def tile_picked_ema_tanh_e_kernel(tc, xT, mem, w1, old, new, offs, slot, out):
         old_last = spread(SLICES - 2, 2, "old_last")
         old_fused = held.tile([P, S - PLAIN], F32, name="old_fused", align_bytes=64)
         nc.vector.tensor_copy(old_fused[:], old_last[:, PLAIN - HALF : S - HALF])
-        old_all = spread(0, SLICES - 1, "old_all")
+        old_all = spread(0, SLICES - 2, "old_all")
         new_all = spread(SLICES, SLICES, "new_all")
 
         def entries(lst, a, b):
@@ -111,7 +111,7 @@ def tile_picked_ema_tanh_e_kernel(tc, xT, mem, w1, old, new, offs, slot, out):
         w_grouped = [held.tile([P, PACK * M], BF16, name=f"w_grouped{z}", tag=f"w_grouped{z}", align_bytes=64) for z in range(PASSES)]
         w_codes = [held.tile([P, M], U32, name=f"w_codes{z}", align_bytes=64) for z in range(PASSES)]
         w_scales = [held.tile([P, M], U8, name=f"w_scales{z}", align_bytes=64) for z in range(PASSES)]
-        parts = [(0, HALF), (HALF, S - SLICE), (S - SLICE, S)]
+        parts = [(0, HALF), (HALF, S)]
         acc = [banks.tile([P, b - a], F32, name=f"acc{a}") for a, b in parts]
 
         def picked(z, t, a, b):
@@ -135,16 +135,16 @@ def tile_picked_ema_tanh_e_kernel(tc, xT, mem, w1, old, new, offs, slot, out):
         def quantize_x(z, a, b):
             quantize(x_codes[z, a, b], x_scales[z][:, a:b], grouped[z, a, b])
 
-        def multiply(z, s):
-            a, b = parts[s]
+        def multiply(z, a, b, closes):
+            base = a - a % HALF
             nc.tensor.matmul_mx(
-                out=acc[s][:],
+                out=acc[a // HALF][:, a - base : b - base],
                 lhsT=w_codes[z][:].bitcast(FP8X4),
                 lhsT_scale=w_scales[z][:],
                 rhs=x_codes[z, a, b].bitcast(FP8X4),
                 rhs_scale=x_scales[z][:, a:b],
                 start=(z == 0),
-                stop=(z == PASSES - 1),
+                stop=closes,
             )
 
         def prepare_w(z):
@@ -171,13 +171,12 @@ def tile_picked_ema_tanh_e_kernel(tc, xT, mem, w1, old, new, offs, slot, out):
             gather_rows(1, t, SLICE, S)
         nc.vector.tensor_copy(rows[1][:, last, SLICE:HALF], picked(1, last, SLICE, HALF))
         nc.vector.tensor_copy(first[:, :, last], picked(1, last, 0, SLICE))
-        gather_rows(1, last, HALF, tail)
-        gather_rows(1, last, tail, S)
-        interleave_rows(1, HALF, tail)
+        gather_rows(1, last, HALF, S)
         nc.vector.tensor_copy(*interleaved(grouped[1, 0, HALF][:, PACK * SLICE :], rows[1][:, :, SLICE:HALF]))
+        interleave_rows(1, HALF, tail)
         prepare_w(0)
-        for s in range(len(parts)):
-            multiply(0, s)
+        for a, b in parts:
+            multiply(0, a, b, False)
         hold_codes(1, 0, HALF, "w_raw0")
         quantize_x(1, 0, HALF)
         hold_grouped(1, tail, S, "w_grouped0")
@@ -188,8 +187,9 @@ def tile_picked_ema_tanh_e_kernel(tc, xT, mem, w1, old, new, offs, slot, out):
         hold_codes(1, HALF, S, "w_raw1")
         quantize_x(1, HALF, tail)
         quantize_x(1, tail, S)
-        for s in range(len(parts)):
-            multiply(1, s)
+        multiply(1, 0, HALF, True)
+        multiply(1, HALF, tail, False)
+        multiply(1, tail, S, True)
 
         found = held.tile([P, PLAIN], F32, name="found", align_bytes=64)
         kept = held.tile([P, S], F32, name="kept", tag="grouped1_2", align_bytes=64)

@@ -19,13 +19,14 @@ COPY = mybir.ActivationFunctionType.Copy
 
 P = 128
 PACK = 4
+PAIR = 2
 PASSES = K // (P * PACK)
 LIST = 16
 SLICE = 128
 SLICES = S // SLICE
 HALF = S // 2
+TAIL = S - SLICE
 RUN = 4
-PLAIN = 256
 LEAD = 448
 
 
@@ -35,16 +36,22 @@ def tile_picked_ema_tanh_e_kernel(tc, xT, mem, w1, old, new, offs, slot, out):
         held = ctx.enter_context(tc.tile_pool(name="held", bufs=1))
         banks = ctx.enter_context(tc.psum_pool(name="banks", bufs=1))
 
+        def sbuf(name, columns, dtype, tag=None):
+            return held.tile([P, columns], dtype, name=name, tag=tag or name, align_bytes=64)
+
         offs_t = held.tile([P, S // LIST], U16, name="offs_t")
         slot_t = held.tile([P, S // LIST], U16, name="slot_t")
-        mem_t = held.tile([P, U], F32, name="mem_t", align_bytes=64)
-        weights = held.tile([P, P], F32, name="weights", align_bytes=64)
-        ident = held.tile([P, P], F32, name="ident", align_bytes=64)
+        mem_t = sbuf("mem_t", U, F32)
+        weights = sbuf("weights", P, F32)
+        ident = sbuf("ident", P, F32)
+        zero = held.tile([P, 1], F32, name="zero")
+        nc.gpsimd.memset(zero[:], 0.0)
+        nc.gpsimd.memset(weights[0 : P // 2, :], 0.0)
+        nc.scalar.activation(weights[P // 2 :, :], zero[P // 2 :, :].to_broadcast([P // 2, P]), COPY)
 
         x_rows = xT.rearrange("(z p t) n -> z p t n", z=PASSES, p=P, t=PACK)
         w_rows = w1.rearrange("(z p t) m -> z p t m", z=PASSES, p=P, t=PACK)
         plane = {}
-        w_raw = {}
 
         def load_planes(z, t, count):
             raw = held.tile([P, count, T], F32, name=f"raw{z}{t}", align_bytes=64)
@@ -52,28 +59,20 @@ def tile_picked_ema_tanh_e_kernel(tc, xT, mem, w1, old, new, offs, slot, out):
             for i in range(count):
                 plane[z, t + i] = raw[:, i, :]
 
-        def load_w(z):
-            w_raw[z] = held.tile([P, PACK, M], F32, name=f"w_raw{z}", tag=f"w_raw{z}", align_bytes=64)
-            nc.sync.dma_start(w_raw[z][:], w_rows[z])
-
-        zero = held.tile([P, 1], F32, name="zero")
-        nc.gpsimd.memset(zero[:], 0.0)
-        nc.gpsimd.memset(weights[0 : P // 2, :], 0.0)
-        nc.scalar.activation(weights[P // 2 :, :], zero[P // 2 :, :].to_broadcast([P // 2, P]), COPY)
-        load_planes(0, 0, 2)
+        load_planes(0, 0, PAIR)
         nc.sync.dma_start(offs_t[:], offs)
         for r, vec in enumerate((old, new)):
             nc.sync.dma_start(weights[r * SLICES : (r + 1) * SLICES, :], vec[0:1, :].rearrange("o (c n) -> (o c) n", n=SLICE))
-        load_planes(0, 2, 2)
+        load_planes(0, PAIR, PAIR)
         for t in range(PACK):
             load_planes(1, t, 1)
         nc.sync.dma_start(slot_t[:], slot)
-        load_w(0)
-        load_w(1)
+        w_raw = [sbuf(f"w_raw{z}", PACK * M, F32) for z in range(PASSES)]
+        for z in range(PASSES):
+            nc.sync.dma_start(w_raw[z][:].rearrange("p (t m) -> p t m", t=PACK), w_rows[z])
         nc.sync.dma_start(mem_t[:], mem)
 
         make_identity(nc, ident[:])
-
         turned = banks.tile([P, P], F32, name="turned")
         nc.tensor.transpose(turned[:], weights[:], ident[:])
         columns = held.tile([P, 2 * SLICES], F32, name="columns")
@@ -86,128 +85,114 @@ def tile_picked_ema_tanh_e_kernel(tc, xT, mem, w1, old, new, offs, slot, out):
                 nc.tensor.transpose(bank[:, c * SLICE : (c + 1) * SLICE], column.to_broadcast([P, P]), ident[:])
             return bank
 
-        old_last = spread(SLICES - 2, 2, "old_last")
-        old_fused = held.tile([P, S - PLAIN], F32, name="old_fused", align_bytes=64)
-        nc.vector.tensor_copy(old_fused[:], old_last[:, PLAIN - HALF : S - HALF])
-        old_all = spread(0, SLICES - 2, "old_all")
+        old_second = spread(SLICES // 2, SLICES // 2, "old_second")
+        old_fused = sbuf("old_fused", HALF, F32)
+        nc.vector.tensor_copy(old_fused[:], old_second[:, 0:HALF])
+        old_first = spread(0, SLICES // 2, "old_first")
         new_all = spread(SLICES, SLICES, "new_all")
 
         def entries(lst, a, b):
             return lst[:, a // LIST : b // LIST]
 
-        def interleaved(dst, src):
-            return (
-                dst.rearrange("p (c i t) -> p c t i", i=RUN, t=PACK),
-                src.rearrange("p t (c i) -> p c t i", i=RUN),
+        def picked(z, t, a, b):
+            return plane[z, t].indirect(entries(offs_t, a, b))
+
+        def weave(copy, dst, src, t, count):
+            copy(
+                dst.rearrange("p (c i t) -> p c t i", i=RUN, t=PACK)[:, :, t : t + count, :],
+                src[:, t : t + count, :].rearrange("p t (c i) -> p c t i", i=RUN),
             )
 
         def quantize(codes, scales, src):
             nc.vector.quantize_mx(out=codes.bitcast(FP8X4), scales=scales, in_=src)
 
         rows = [held.tile([P, PACK, S], (F32, BF16)[z], name=f"rows{z}", align_bytes=64) for z in range(PASSES)]
-        grouped = {}
+        grouped = {(0, a, a + HALF): sbuf(f"grouped0_{a}", PACK * HALF, BF16) for a in (0, HALF)}
+        grouped[1, 0, HALF] = sbuf("grouped1_0", PACK * HALF, BF16)
+        grouped[1, HALF, TAIL] = sbuf("grouped1_2", PACK * SLICE, BF16)
+        x_scales = [sbuf(f"x_scales{z}", S, U8) for z in range(PASSES)]
         x_codes = {}
-        x_scales = [held.tile([P, S], U8, name=f"x_scales{z}", align_bytes=64) for z in range(PASSES)]
-        w_grouped = [held.tile([P, PACK * M], BF16, name=f"w_grouped{z}", tag=f"w_grouped{z}", align_bytes=64) for z in range(PASSES)]
-        w_codes = [held.tile([P, M], U32, name=f"w_codes{z}", align_bytes=64) for z in range(PASSES)]
-        w_scales = [held.tile([P, M], U8, name=f"w_scales{z}", align_bytes=64) for z in range(PASSES)]
-        parts = [(0, HALF), (HALF, S)]
-        acc = [banks.tile([P, b - a], F32, name=f"acc{a}") for a, b in parts]
+        w_grouped = [sbuf(f"w_grouped{z}", PACK * M, BF16) for z in range(PASSES)]
+        w_codes = [sbuf(f"w_codes{z}", M, U32) for z in range(PASSES)]
+        w_scales = [sbuf(f"w_scales{z}", M, U8) for z in range(PASSES)]
+        acc = {a: banks.tile([P, HALF], F32, name=f"acc{a}") for a in (0, HALF)}
 
-        def picked(z, t, a, b):
-            return plane[z, t].indirect(entries(offs_t, a, b))
+        def words(z, a, b):
+            base, end = [(lo, hi) for y, lo, hi in grouped if y == z and lo <= a < hi][0]
+            return grouped[z, base, end][:, PACK * (a - base) : PACK * (b - base)]
 
-        def gather_rows(z, t, a, b):
-            nc.scalar.activation(rows[z][:, t, a:b], picked(z, t, a, b), COPY)
+        def weave_x(copy, z, u, a, b):
+            weave(copy, words(z, a, b), rows[z][:, :, a:b], PAIR * u, PAIR)
 
-        def hold_grouped(z, a, b, tag):
-            grouped[z, a, b] = held.tile([P, PACK * (b - a)], BF16, name=f"grouped{z}_{a}", tag=tag, align_bytes=64)[:]
+        def quantize_x(z, a, b, tag):
+            x_codes[z, a, b] = sbuf(f"x_codes{z}_{a}", b - a, U32, tag)
+            quantize(x_codes[z, a, b][:], x_scales[z][:, a:b], words(z, a, b))
 
-        def interleave_rows(z, a, b):
-            nc.vector.tensor_copy(*interleaved(grouped[z, a, b], rows[z][:, :, a:b]))
-
-        def hold_codes(z, a, b, tag):
-            tile = held.tile([P, b - a], U32, name=f"x_codes{z}_{a}", tag=tag, align_bytes=64)
-            for c in range(a, b, SLICE):
-                x_codes[z, c, c + SLICE] = tile[:, c - a : c - a + SLICE]
-            x_codes[z, a, b] = tile[:]
-
-        def quantize_x(z, a, b):
-            quantize(x_codes[z, a, b], x_scales[z][:, a:b], grouped[z, a, b])
+        def prepare_w(z):
+            weave(nc.scalar.copy, w_grouped[z][:], w_raw[z][:].rearrange("p (t m) -> p t m", t=PACK), 0, PACK)
+            quantize(w_codes[z][:], w_scales[z][:], w_grouped[z][:])
 
         def multiply(z, a, b, closes):
             base = a - a % HALF
             nc.tensor.matmul_mx(
-                out=acc[a // HALF][:, a - base : b - base],
+                out=acc[base][:, a - base : b - base],
                 lhsT=w_codes[z][:].bitcast(FP8X4),
                 lhsT_scale=w_scales[z][:],
-                rhs=x_codes[z, a, b].bitcast(FP8X4),
+                rhs=x_codes[z, a, b][:].bitcast(FP8X4),
                 rhs_scale=x_scales[z][:, a:b],
                 start=(z == 0),
                 stop=closes,
             )
 
-        def prepare_w(z):
-            nc.scalar.copy(*interleaved(w_grouped[z][:], w_raw[z][:]))
-            quantize(w_codes[z][:], w_scales[z][:], w_grouped[z][:])
-
-        for t in range(PACK):
-            nc.vector.tensor_copy(rows[0][:, t, 0:HALF], picked(0, t, 0, HALF))
-            gather_rows(0, t, HALF, S)
+        for u in range(PACK // PAIR):
+            for t in range(PAIR * u, PAIR * (u + 1)):
+                nc.vector.tensor_copy(rows[0][:, t, 0:HALF], picked(0, t, 0, HALF))
+                nc.scalar.activation(rows[0][:, t, HALF:S], picked(0, t, HALF, S), COPY)
+            weave_x(nc.vector.tensor_copy, 0, u, 0, HALF)
+            weave_x((nc.scalar.copy, nc.vector.tensor_copy)[u], 0, u, HALF, S)
         for a in (0, HALF):
-            hold_grouped(0, a, a + HALF, f"grouped0_{a}")
-            interleave_rows(0, a, a + HALF)
-        for a in (0, HALF):
-            hold_codes(0, a, a + HALF, f"codes0_{a}")
-            quantize_x(0, a, a + HALF)
+            quantize_x(0, a, a + HALF, None)
 
-        tail = S - SLICE
         last = PACK - 1
-        hold_grouped(1, 0, HALF, "grouped1_0")
-        hold_grouped(1, HALF, tail, "grouped1_2")
-        first = grouped[1, 0, HALF][:, 0 : PACK * SLICE].rearrange("p (j t) -> p j t", t=PACK)
+        first = words(1, 0, SLICE).rearrange("p (j t) -> p j t", t=PACK)
         for t in range(last):
             nc.vector.tensor_copy(first[:, :, t], picked(1, t, 0, SLICE))
-            gather_rows(1, t, SLICE, S)
+            nc.scalar.activation(rows[1][:, t, SLICE:S], picked(1, t, SLICE, S), COPY)
+            if t == PAIR - 1:
+                weave_x(nc.vector.tensor_copy, 1, 0, SLICE, HALF)
         nc.vector.tensor_copy(rows[1][:, last, SLICE:HALF], picked(1, last, SLICE, HALF))
         nc.vector.tensor_copy(first[:, :, last], picked(1, last, 0, SLICE))
-        gather_rows(1, last, HALF, S)
-        nc.vector.tensor_copy(*interleaved(grouped[1, 0, HALF][:, PACK * SLICE :], rows[1][:, :, SLICE:HALF]))
-        interleave_rows(1, HALF, tail)
+        nc.scalar.activation(rows[1][:, last, HALF:S], picked(1, last, HALF, S), COPY)
+        weave_x(nc.vector.tensor_copy, 1, 1, SLICE, HALF)
+        weave(nc.vector.tensor_copy, words(1, HALF, TAIL), rows[1][:, :, HALF:TAIL], 0, PACK)
         prepare_w(0)
-        for a, b in parts:
-            multiply(0, a, b, False)
-        hold_codes(1, 0, HALF, "w_raw0")
-        quantize_x(1, 0, HALF)
-        hold_grouped(1, tail, S, "w_grouped0")
-        cut = PACK * (LEAD - tail)
-        nc.vector.tensor_copy(*interleaved(grouped[1, tail, S][:, 0:cut], rows[1][:, :, tail:LEAD]))
+        for a in (0, HALF):
+            multiply(0, a, a + HALF, False)
+        quantize_x(1, 0, HALF, "w_raw0")
+        grouped[1, TAIL, S] = sbuf("grouped1_3", PACK * SLICE, BF16, "w_grouped0")
+        weave(nc.vector.tensor_copy, words(1, TAIL, LEAD), rows[1][:, :, TAIL:LEAD], 0, PACK)
         prepare_w(1)
-        nc.scalar.copy(*interleaved(grouped[1, tail, S][:, cut:], rows[1][:, :, LEAD:S]))
-        hold_codes(1, HALF, S, "w_raw1")
-        quantize_x(1, HALF, tail)
-        quantize_x(1, tail, S)
+        weave(nc.scalar.copy, words(1, LEAD, S), rows[1][:, :, LEAD:S], 0, PACK)
+        quantize_x(1, HALF, TAIL, "w_raw1")
+        quantize_x(1, TAIL, S, None)
         multiply(1, 0, HALF, True)
-        multiply(1, HALF, tail, False)
-        multiply(1, tail, S, True)
+        multiply(1, HALF, TAIL, False)
+        multiply(1, TAIL, S, True)
 
-        found = held.tile([P, PLAIN], F32, name="found", align_bytes=64)
-        kept = held.tile([P, S], F32, name="kept", tag="grouped1_2", align_bytes=64)
-        moved = held.tile([P, S], F32, name="moved", align_bytes=64)
+        found = sbuf("found", HALF, F32)
+        kept = sbuf("kept", S, F32, "grouped1_2")
+        moved = sbuf("moved", S, F32)
+        y = sbuf("y", S, F32)
 
         def window(a, b):
             return mem_t[:].indirect(entries(slot_t, a, b))
 
-        def weigh(a, b):
-            nc.vector.tensor_tensor(moved[:, a:b], y[:, a:b], new_all[:, a:b], MULT)
-
-        nc.scalar.activation(found[:], window(0, PLAIN), COPY)
-        nc.vector.tensor_tensor(kept[:, PLAIN:S], window(PLAIN, S), old_fused[:], MULT)
-        nc.vector.tensor_tensor(kept[:, 0:PLAIN], found[:], old_all[:, 0:PLAIN], MULT)
-        y = held.tile([P, S], F32, name="y", align_bytes=64)
-        for s, (a, b) in enumerate(parts):
-            nc.scalar.activation(y[:, a:b], acc[s][:], TANH)
-        weigh(0, HALF)
-        weigh(HALF, S)
+        nc.scalar.activation(found[:], window(0, HALF), COPY)
+        nc.vector.tensor_tensor(kept[:, HALF:S], window(HALF, S), old_fused[:], MULT)
+        nc.vector.tensor_tensor(kept[:, 0:HALF], found[:], old_first[:, 0:HALF], MULT)
+        for a in (0, HALF):
+            nc.scalar.activation(y[:, a : a + HALF], acc[a][:], TANH)
+        for a in (0, HALF):
+            nc.vector.tensor_tensor(moved[:, a : a + HALF], y[:, a : a + HALF], new_all[:, a : a + HALF], MULT)
         nc.vector.tensor_tensor(window(0, S), moved[:], kept[:], ADD)
         nc.sync.dma_start(out, mem_t[:])

from contextlib import ExitStack

import concourse.mybir as mybir
from concourse.masks import make_identity

K, T, S, M, U = 1024, 1024, 512, 128, 1024
FLOPS = 2 * K * M * S

F32 = mybir.dt.float32
BF16 = mybir.dt.bfloat16
U32 = mybir.dt.uint32
U16 = mybir.dt.uint16
U8 = mybir.dt.uint8
FP8X4 = mybir.dt.float8_e4m3fn_x4
MULT = mybir.AluOpType.mult
ADD = mybir.AluOpType.add
TANH = mybir.ActivationFunctionType.Tanh
COPY = mybir.ActivationFunctionType.Copy

P = 128
PACK = 4
PAIR = 2
PASSES = K // (P * PACK)
LIST = 16
SLICE = 128
SLICES = S // SLICE
HALF = S // 2
TAIL = S - SLICE
RUN = 4
LEAD = 448


def tile_picked_ema_tanh_e_kernel(tc, xT, mem, w1, old, new, offs, slot, out):
    nc = tc.nc
    with ExitStack() as ctx:
        held = ctx.enter_context(tc.tile_pool(name="held", bufs=1))
        banks = ctx.enter_context(tc.psum_pool(name="banks", bufs=1))

        def sbuf(name, columns, dtype, tag=None):
            return held.tile([P, columns], dtype, name=name, tag=tag or name, align_bytes=64)

        offs_t = held.tile([P, S // LIST], U16, name="offs_t")
        slot_t = held.tile([P, S // LIST], U16, name="slot_t")
        mem_t = sbuf("mem_t", U, F32)
        weights = sbuf("weights", P, F32)
        ident = sbuf("ident", P, F32)
        zero = held.tile([P, 1], F32, name="zero")
        nc.gpsimd.memset(zero[:], 0.0)
        nc.gpsimd.memset(weights[0 : P // 2, :], 0.0)
        nc.scalar.activation(weights[P // 2 :, :], zero[P // 2 :, :].to_broadcast([P // 2, P]), COPY)

        x_rows = xT.rearrange("(z p t) n -> z p t n", z=PASSES, p=P, t=PACK)
        w_rows = w1.rearrange("(z p t) m -> z p t m", z=PASSES, p=P, t=PACK)
        plane = {}

        def load_planes(z, t, count):
            raw = held.tile([P, count, T], F32, name=f"raw{z}{t}", align_bytes=64)
            nc.sync.dma_start(raw[:], x_rows[z][:, t : t + count, :])
            for i in range(count):
                plane[z, t + i] = raw[:, i, :]

        load_planes(0, 0, PAIR)
        nc.sync.dma_start(offs_t[:], offs)
        for r, vec in enumerate((old, new)):
            nc.sync.dma_start(weights[r * SLICES : (r + 1) * SLICES, :], vec[0:1, :].rearrange("o (c n) -> (o c) n", n=SLICE))
        load_planes(0, PAIR, PAIR)
        for t in range(PACK):
            load_planes(1, t, 1)
        nc.sync.dma_start(slot_t[:], slot)
        w_raw = [sbuf(f"w_raw{z}", PACK * M, F32) for z in range(PASSES)]
        for z in range(PASSES):
            nc.sync.dma_start(w_raw[z][:].rearrange("p (t m) -> p t m", t=PACK), w_rows[z])
        nc.sync.dma_start(mem_t[:], mem)

        make_identity(nc, ident[:])
        turned = banks.tile([P, P], F32, name="turned")
        nc.tensor.transpose(turned[:], weights[:], ident[:])
        columns = held.tile([P, 2 * SLICES], F32, name="columns")
        nc.scalar.copy(columns[:], turned[:, 0 : 2 * SLICES])

        def spread(first, count, name):
            bank = banks.tile([P, S], F32, name=name)
            for c in range(count):
                column = columns[:, first + c : first + c + 1]
                nc.tensor.transpose(bank[:, c * SLICE : (c + 1) * SLICE], column.to_broadcast([P, P]), ident[:])
            return bank

        old_second = spread(SLICES // 2, SLICES // 2, "old_second")
        old_fused = sbuf("old_fused", HALF, F32)
        nc.vector.tensor_copy(old_fused[:], old_second[:, 0:HALF])
        old_first = spread(0, SLICES // 2, "old_first")
        new_all = spread(SLICES, SLICES, "new_all")

        def entries(lst, a, b):
            return lst[:, a // LIST : b // LIST]

        def picked(z, t, a, b):
            return plane[z, t].indirect(entries(offs_t, a, b))

        def weave(copy, dst, src, t, count):
            copy(
                dst.rearrange("p (c i t) -> p c t i", i=RUN, t=PACK)[:, :, t : t + count, :],
                src[:, t : t + count, :].rearrange("p t (c i) -> p c t i", i=RUN),
            )

        def quantize(codes, scales, src):
            nc.vector.quantize_mx(out=codes.bitcast(FP8X4), scales=scales, in_=src)

        rows = [held.tile([P, PACK, S], (F32, BF16)[z], name=f"rows{z}", align_bytes=64) for z in range(PASSES)]
        grouped = {(0, a, a + HALF): sbuf(f"grouped0_{a}", PACK * HALF, BF16) for a in (0, HALF)}
        grouped[1, 0, HALF] = sbuf("grouped1_0", PACK * HALF, BF16)
        grouped[1, HALF, TAIL] = sbuf("grouped1_2", PACK * SLICE, BF16)
        x_scales = [sbuf(f"x_scales{z}", S, U8) for z in range(PASSES)]
        x_codes = {}
        w_grouped = [sbuf(f"w_grouped{z}", PACK * M, BF16) for z in range(PASSES)]
        w_codes = [sbuf(f"w_codes{z}", M, U32) for z in range(PASSES)]
        w_scales = [sbuf(f"w_scales{z}", M, U8) for z in range(PASSES)]
        acc = {a: banks.tile([P, HALF], F32, name=f"acc{a}") for a in (0, HALF)}

        def words(z, a, b):
            base, end = [(lo, hi) for y, lo, hi in grouped if y == z and lo <= a < hi][0]
            return grouped[z, base, end][:, PACK * (a - base) : PACK * (b - base)]

        def weave_x(copy, z, u, a, b):
            weave(copy, words(z, a, b), rows[z][:, :, a:b], PAIR * u, PAIR)

        def quantize_x(z, a, b, tag):
            x_codes[z, a, b] = sbuf(f"x_codes{z}_{a}", b - a, U32, tag)
            quantize(x_codes[z, a, b][:], x_scales[z][:, a:b], words(z, a, b))

        def prepare_w(z):
            weave(nc.scalar.copy, w_grouped[z][:], w_raw[z][:].rearrange("p (t m) -> p t m", t=PACK), 0, PACK)
            quantize(w_codes[z][:], w_scales[z][:], w_grouped[z][:])

        def multiply(z, a, b, closes):
            base = a - a % HALF
            nc.tensor.matmul_mx(
                out=acc[base][:, a - base : b - base],
                lhsT=w_codes[z][:].bitcast(FP8X4),
                lhsT_scale=w_scales[z][:],
                rhs=x_codes[z, a, b][:].bitcast(FP8X4),
                rhs_scale=x_scales[z][:, a:b],
                start=(z == 0),
                stop=closes,
            )

        for u in range(PACK // PAIR):
            for t in range(PAIR * u, PAIR * (u + 1)):
                nc.vector.tensor_copy(rows[0][:, t, 0:HALF], picked(0, t, 0, HALF))
                nc.scalar.activation(rows[0][:, t, HALF:S], picked(0, t, HALF, S), COPY)
            weave_x(nc.vector.tensor_copy, 0, u, 0, HALF)
            weave_x((nc.scalar.copy, nc.vector.tensor_copy)[u], 0, u, HALF, S)
        for a in (0, HALF):
            quantize_x(0, a, a + HALF, None)

        last = PACK - 1
        first = words(1, 0, SLICE).rearrange("p (j t) -> p j t", t=PACK)
        for t in range(last):
            nc.vector.tensor_copy(first[:, :, t], picked(1, t, 0, SLICE))
            nc.scalar.activation(rows[1][:, t, SLICE:S], picked(1, t, SLICE, S), COPY)
            if t == PAIR - 1:
                weave_x(nc.vector.tensor_copy, 1, 0, SLICE, HALF)
        nc.vector.tensor_copy(rows[1][:, last, SLICE:HALF], picked(1, last, SLICE, HALF))
        nc.vector.tensor_copy(first[:, :, last], picked(1, last, 0, SLICE))
        nc.scalar.activation(rows[1][:, last, HALF:S], picked(1, last, HALF, S), COPY)
        weave_x(nc.vector.tensor_copy, 1, 1, SLICE, HALF)
        weave(nc.vector.tensor_copy, words(1, HALF, TAIL), rows[1][:, :, HALF:TAIL], 0, PACK)
        prepare_w(0)
        for a in (0, HALF):
            multiply(0, a, a + HALF, False)
        quantize_x(1, 0, HALF, "w_raw0")
        grouped[1, TAIL, S] = sbuf("grouped1_3", PACK * SLICE, BF16, "w_grouped0")
        weave(nc.vector.tensor_copy, words(1, TAIL, LEAD), rows[1][:, :, TAIL:LEAD], 0, PACK)
        prepare_w(1)
        weave(nc.scalar.copy, words(1, LEAD, S), rows[1][:, :, LEAD:S], 0, PACK)
        quantize_x(1, HALF, TAIL, "w_raw1")
        quantize_x(1, TAIL, S, None)
        multiply(1, 0, HALF, True)
        multiply(1, HALF, TAIL, False)
        multiply(1, TAIL, S, True)

        found = sbuf("found", HALF, F32)
        kept = sbuf("kept", S, F32, "grouped1_2")
        moved = sbuf("moved", S, F32)
        y = sbuf("y", S, F32)

        def window(a, b):
            return mem_t[:].indirect(entries(slot_t, a, b))

        nc.scalar.activation(found[:], window(0, HALF), COPY)
        nc.vector.tensor_tensor(kept[:, HALF:S], window(HALF, S), old_fused[:], MULT)
        nc.vector.tensor_tensor(kept[:, 0:HALF], found[:], old_first[:, 0:HALF], MULT)
        for a in (0, HALF):
            nc.scalar.activation(y[:, a : a + HALF], acc[a][:], TANH)
        for a in (0, HALF):
            nc.vector.tensor_tensor(moved[:, a : a + HALF], y[:, a : a + HALF], new_all[:, a : a + HALF], MULT)
        nc.vector.tensor_tensor(window(0, S), moved[:], kept[:], ADD)
        nc.sync.dma_start(out, mem_t[:])
